import numpy as np
import ml_dtypes


def mxq(x, axis, fmt="e4m3"):
    dtype, down = {"e4m3": (ml_dtypes.float8_e4m3fn, 7), "e5m2": (ml_dtypes.float8_e5m2, 14)}[fmt]
    v = np.moveaxis(np.asarray(x, np.float32).astype(ml_dtypes.bfloat16).astype(np.float64), axis, -1)
    blocks = v.reshape(v.shape[:-1] + (-1, 32))
    amax = np.abs(blocks).max(-1, keepdims=True)
    byte = np.maximum(np.where(amax > 0, np.frexp(amax)[1] - 1 + 127, 0) - down, 1)
    scale = np.exp2(byte - 127.0)
    codes = (blocks / scale).astype(np.float32).astype(dtype).astype(np.float64)
    return np.moveaxis((codes * scale).reshape(v.shape), -1, axis)


WIDE = False


def mx_kscale(k):
    if not WIDE:
        return np.ones(k)
    levels = np.array([10, -10, 5, -5, 0])
    if k % 512:
        return np.exp2(np.random.permutation(np.resize(levels, k // 32))).repeat(32)
    a = np.empty((k // 512, 16))
    for p in range(k // 512):
        a[p, :8] = np.random.permutation(np.resize(levels, 8))
        for g in range(8):
            far = levels[np.abs(levels - a[p, g]) >= 10]
            a[p, g + 8] = far[np.random.randint(len(far))]
    return np.exp2(a.ravel()).repeat(32)


def f64(x):
    return np.asarray(x).astype(np.float64)


def striped(idx):
    return np.tile(idx.reshape(-1, 16).T, (8, 1)).astype(np.uint16)


def unstriped(offs):
    return offs[:16].T.reshape(-1).astype(np.int64)


def pack_weight(w):
    k, n = w.shape
    w = f64(np.asarray(w, np.float32).astype(ml_dtypes.bfloat16)).reshape(k // 32, 32, n)
    amax = np.abs(w).max(1)
    byte = np.clip(np.where(amax > 0, np.frexp(amax)[1] - 1 + 127 - 7, 1), 1, 254)
    scaled = (w * np.exp2(127.0 - byte)[:, None, :]).reshape(k, n).astype(np.float32)
    words = np.ascontiguousarray(scaled.reshape(k // 512, 128, 4, n).transpose(0, 1, 3, 2)).astype(ml_dtypes.float8_e4m3fn).view(np.uint8)
    return words, np.ascontiguousarray(byte.astype(np.uint8).reshape(k // 512, 16, n))


def unpack_weight(words, scales):
    g, p, n, _ = words.shape
    vals = np.ascontiguousarray(words).view(ml_dtypes.float8_e4m3fn).astype(np.float64) * np.repeat(np.exp2(scales.astype(np.float64) - 127.0), 8, axis=1)[..., None]
    return vals.transpose(0, 1, 3, 2).reshape(g * 512, n)


def gelu(v):
    return 0.5 * v * (1.0 + np.tanh(np.sqrt(2.0 / np.pi) * (v + 0.044715 * v**3)))


K, T, S, N = 512, 2048, 512, 512


def setup_inputs():
    n = np.random.standard_normal
    s = mx_kscale(K)[:, None]
    w1, w2 = n((2, K, N)) / np.sqrt(2 * K) / s[None]
    p1, p2 = pack_weight(w1), pack_weight(w2)
    return {
        "xT": (n((K, S)) * s).astype(np.float32),
        "sT": (n((K, T)) * s).astype(np.float32),
        "w1_words": p1[0],
        "w1_scales": p1[1],
        "w2_words": p2[0],
        "w2_scales": p2[1],
        "b": (0.3 * n((N, 1))).astype(np.float32),
        "offs": striped(np.random.permutation(T)[:S]),
    }


def reference(xT, sT, w1_words, w1_scales, w2_words, w2_scales, b, offs):
    y = unpack_weight(w1_words, w1_scales).T @ mxq(f64(xT), 0, "e4m3") + unpack_weight(w2_words, w2_scales).T @ mxq(f64(sT)[:, unstriped(offs)], 0, "e4m3")
    return gelu(y + f64(b))

@@ -1,0 +1,146 @@
+from contextlib import ExitStack
+
+import concourse.mybir as mybir
+from concourse.masks import make_identity
+
+P = 128
+K = 512
+T = 2048
+S = 512
+N = 512
+PACK = 4
+HALF = 256
+M_TILES = N // P
+FLOPS = 2 * 2 * K * N * S
+
+F32 = mybir.dt.float32
+BF16 = mybir.dt.bfloat16
+I32 = mybir.dt.int32
+U32 = mybir.dt.uint32
+U16 = mybir.dt.uint16
+U8 = mybir.dt.uint8
+FP8X4 = mybir.dt.float8_e4m3fn_x4
+GELU = mybir.ActivationFunctionType.Gelu_apprx_tanh
+
+
+def tile_picked_recall_gelu_e_kernel(tc, xT, sT, w1_words, w1_scales, w2_words, w2_scales, b, offs, out):
+    nc = tc.nc
+    with ExitStack() as ctx:
+        held = ctx.enter_context(tc.tile_pool(name="held", bufs=1))
+        psum = ctx.enter_context(tc.psum_pool(name="psum", bufs=1))
+
+        offsets = held.tile([P, S // 16], U16, name="offsets")
+        planes = [held.tile([P, T], F32, name="plane%d" % t, align_bytes=64) for t in range(PACK)]
+        words1 = held.tile([P, N], I32, name="words1", align_bytes=64)
+        words2 = held.tile([P, N], I32, name="words2", align_bytes=64)
+        scales1 = held.tile([P, N], U8, name="scales1", align_bytes=64)
+        scales2 = held.tile([P, N], U8, name="scales2", align_bytes=64)
+        bias_rows = held.tile([P, P], F32, name="bias_rows")
+        bias = held.tile([P, M_TILES], F32, name="bias")
+        ident = held.tile([P, P], F32, name="ident")
+        dummy = held.tile([P, 2], F32, name="dummy")
+
+        s_rows = sT.rearrange("(p t) c -> t p c", t=PACK)
+        x_rows = xT.rearrange("(p j) n -> p j n", j=PACK)
+
+        nc.gpsimd.memset(scales1[:].bitcast(I32), 0)
+        nc.vector.memset(scales2[:].bitcast(I32), 0)
+        nc.vector.memset(dummy[:], 0.0)
+        nc.vector.memset(bias_rows[:], 0.0)
+        make_identity(nc, ident[:])
+
+        pieces = ((0, 256), (256, 128), (384, 128))
+        x_raw = [held.tile([P, PACK, n], F32, name="x_raw%d" % c, align_bytes=64) for c, n in pieces]
+
+        def load_scale_rows(queue, scales, source):
+            for q in range(4):
+                queue.dma_start(
+                    scales[32 * q : 32 * q + 4, :].bitcast(I32),
+                    source[0, 4 * q : 4 * q + 4, :].bitcast(I32),
+                )
+
+        def load_x(i):
+            c, n = pieces[i]
+            nc.sync.dma_start(x_raw[i][:], x_rows[:, :, c : c + n])
+
+        nc.sync.dma_start(planes[0][:], s_rows[0])
+        nc.sync.dma_start(offsets[:], offs)
+        nc.sync.dma_start(planes[1][:], s_rows[1])
+        load_scale_rows(nc.scalar, scales1, w1_scales)
+        nc.sync.dma_start(planes[2][:], s_rows[2])
+        load_scale_rows(nc.gpsimd, scales2, w2_scales)
+        nc.gpsimd.dma_start(bias_rows[0:M_TILES, :], b.rearrange("(m p) o -> m (p o)", p=P))
+        nc.scalar.activation(dummy[:, 1:2], dummy[:, 0:1], GELU)
+        load_x(0)
+        nc.sync.dma_start(planes[3][:], s_rows[3])
+        nc.sync.dma_start(words1[:], w1_words[0].rearrange("p m r -> p (m r)").bitcast(I32))
+        nc.sync.dma_start(words2[:], w2_words[0].rearrange("p m r -> p (m r)").bitcast(I32))
+        load_x(1)
+        load_x(2)
+
+        def quantise(mix, n, name):
+            codes = held.tile([P, n], U32, name=name + "_codes", align_bytes=64)
+            scales = held.tile([P, n], U8, name=name + "_scales", align_bytes=64)
+            nc.vector.quantize_mx(
+                out=codes[:].bitcast(FP8X4), scales=scales[:], in_=mix.rearrange("p n t -> p (n t)")
+            )
+            return codes, scales
+
+        turned = psum.tile([P, P], F32, name="turned", tag="acc7")
+        nc.tensor.transpose(turned[:], bias_rows[:], ident[:])
+        nc.vector.tensor_copy(bias[:], turned[:, 0:M_TILES])
+
+        s_mix = held.tile([P, S, PACK], BF16, name="s_mix", align_bytes=64)
+        for t in range(PACK - 1):
+            nc.vector.tensor_copy(s_mix[:, :, t], planes[t][:].indirect(offsets[:]))
+        mix0 = held.tile([P, 256, PACK], BF16, name="x_mix0", align_bytes=64)
+        nc.scalar.copy(mix0[:], x_raw[0][:].rearrange("p j n -> p n j"))
+        x0_quant = quantise(mix0[:], 256, "x0")
+        for h in range(2):
+            nc.vector.tensor_copy(
+                s_mix[:, h * HALF : (h + 1) * HALF, PACK - 1],
+                planes[PACK - 1][:].indirect(offsets[:, h * 16 : (h + 1) * 16]),
+            )
+        s_quant = [quantise(s_mix[:, h * HALF : (h + 1) * HALF, :], HALF, "s%d" % h) for h in range(2)]
+
+        out_rows = out.rearrange("(m p) n -> p m n", p=P)
+
+        def products(accs, words, scales, moving, lo, n, opens):
+            codes, plane = moving
+            for m in range(M_TILES):
+                nc.tensor.matmul_mx(
+                    out=accs[m][:],
+                    lhsT=words[:, m * P : (m + 1) * P].bitcast(FP8X4),
+                    lhsT_scale=scales[:, m * P : (m + 1) * P],
+                    rhs=codes[:, lo : lo + n].bitcast(FP8X4),
+                    rhs_scale=plane[:, lo : lo + n],
+                    start=opens,
+                    stop=not opens,
+                )
+
+        def banks(i):
+            n = pieces[i][1]
+            return [
+                psum.tile([P, n], F32, name="acc%d_%d" % (i, m), tag="acc%d" % ((i % 2) * M_TILES + m))
+                for m in range(M_TILES)
+            ]
+
+        def leave(i, accs):
+            c, n = pieces[i]
+            for m0 in range(0, M_TILES, 2):
+                result = held.tile([P, 2, n], F32, name="result%d_%d" % (i, m0))
+                for m in (m0, m0 + 1):
+                    nc.scalar.activation(result[:, m - m0, :], accs[m][:], GELU, bias=bias[:, m : m + 1])
+                nc.sync.dma_start(out_rows[:, m0 : m0 + 2, c : c + n], result[:])
+
+        accs = banks(0)
+        products(accs, words1, scales1, x0_quant, 0, 256, True)
+        products(accs, words2, scales2, s_quant[0], 0, 256, False)
+        leave(0, accs)
+        for i in (1, 2):
+            accs = banks(i)
+            products(accs, words2, scales2, s_quant[1], pieces[i][0] - HALF, P, True)
+            mix = held.tile([P, P, PACK], BF16, name="x_mix%d" % i, align_bytes=64)
+            nc.vector.tensor_copy(mix[:], x_raw[i][:].rearrange("p j n -> p n j"))
+            products(accs, words1, scales1, quantise(mix[:], P, "x%d" % i), 0, P, False)
+            leave(i, accs)

@@ -30,31 +30,31 @@ def tile_picked_recall_gelu_e_kernel(tc, xT, sT, w1_words, w1_scales, w2_words, 
         psum = ctx.enter_context(tc.psum_pool(name="psum", bufs=1))
 
         offsets = held.tile([P, S // 16], U16, name="offsets")
-        planes = [held.tile([P, T], F32, name="plane%d" % t, align_bytes=64) for t in range(PACK)]
+        planes01 = held.tile([P, 2, T], F32, name="planes01", align_bytes=64)
+        plane2 = held.tile([P, T], F32, name="plane2", tag="plane2", align_bytes=64)
+        plane3 = held.tile([P, T], F32, name="plane3", align_bytes=64)
         words1 = held.tile([P, N], I32, name="words1", align_bytes=64)
         words2 = held.tile([P, N], I32, name="words2", align_bytes=64)
-        scales1 = held.tile([P, N], U8, name="scales1", align_bytes=64)
-        scales2 = held.tile([P, N], U8, name="scales2", align_bytes=64)
+        w_scales = held.tile([P, 2 * N], U8, name="w_scales", align_bytes=64)
+        scales1 = w_scales[:, 0:N]
+        scales2 = w_scales[:, N : 2 * N]
         bias_rows = held.tile([P, P], F32, name="bias_rows")
-        bias = held.tile([P, M_TILES], F32, name="bias")
         ident = held.tile([P, P], F32, name="ident")
         dummy = held.tile([P, 2], F32, name="dummy")
-
-        s_rows = sT.rearrange("(p t) c -> t p c", t=PACK)
-        x_rows = xT.rearrange("(p j) n -> p j n", j=PACK)
-
-        nc.gpsimd.memset(scales1[:].bitcast(I32), 0)
-        nc.vector.memset(scales2[:].bitcast(I32), 0)
-        nc.vector.memset(dummy[:], 0.0)
-        nc.vector.memset(bias_rows[:], 0.0)
-        make_identity(nc, ident[:])
-
         pieces = ((0, 256), (256, 128), (384, 128))
         x_raw = [held.tile([P, PACK, n], F32, name="x_raw%d" % c, align_bytes=64) for c, n in pieces]
 
-        def load_scale_rows(queue, scales, source):
+        s_rows = sT.rearrange("(p t) c -> p t c", t=PACK)
+        x_rows = xT.rearrange("(p j) n -> p j n", j=PACK)
+
+        nc.gpsimd.memset(w_scales[:].bitcast(I32), 0)
+        nc.gpsimd.memset(bias_rows[:], 0.0)
+        nc.vector.memset(dummy[:], 0.0)
+        make_identity(nc, ident[:])
+
+        def load_scale_rows(scales, source):
             for q in range(4):
-                queue.dma_start(
+                nc.sync.dma_start(
                     scales[32 * q : 32 * q + 4, :].bitcast(I32),
                     source[0, 4 * q : 4 * q + 4, :].bitcast(I32),
                 )
@@ -63,19 +63,21 @@ def tile_picked_recall_gelu_e_kernel(tc, xT, sT, w1_words, w1_scales, w2_words, 
             c, n = pieces[i]
             nc.sync.dma_start(x_raw[i][:], x_rows[:, :, c : c + n])
 
-        nc.sync.dma_start(planes[0][:], s_rows[0])
-        nc.sync.dma_start(offsets[:], offs)
-        nc.sync.dma_start(planes[1][:], s_rows[1])
-        load_scale_rows(nc.scalar, scales1, w1_scales)
-        nc.sync.dma_start(planes[2][:], s_rows[2])
-        load_scale_rows(nc.gpsimd, scales2, w2_scales)
-        nc.gpsimd.dma_start(bias_rows[0:M_TILES, :], b.rearrange("(m p) o -> m (p o)", p=P))
+        def load_words(words, source):
+            nc.sync.dma_start(words[:], source[0].rearrange("p m r -> p (m r)").bitcast(I32))
+
         nc.scalar.activation(dummy[:, 1:2], dummy[:, 0:1], GELU)
+        nc.sync.dma_start(planes01[:], s_rows[:, 0:2, :])
+        nc.sync.dma_start(offsets[:], offs)
+        load_scale_rows(scales1, w1_scales)
         load_x(0)
-        nc.sync.dma_start(planes[3][:], s_rows[3])
-        nc.sync.dma_start(words1[:], w1_words[0].rearrange("p m r -> p (m r)").bitcast(I32))
-        nc.sync.dma_start(words2[:], w2_words[0].rearrange("p m r -> p (m r)").bitcast(I32))
+        nc.sync.dma_start(plane2[:], s_rows[:, 2, :])
+        nc.sync.dma_start(bias_rows[0:M_TILES, :], b.rearrange("(m p) o -> m (p o)", p=P))
+        load_scale_rows(scales2, w2_scales)
+        nc.sync.dma_start(plane3[:], s_rows[:, 3, :])
+        load_words(words1, w1_words)
         load_x(1)
+        load_words(words2, w2_words)
         load_x(2)
 
         def quantise(mix, n, name):
@@ -86,61 +88,71 @@ def tile_picked_recall_gelu_e_kernel(tc, xT, sT, w1_words, w1_scales, w2_words, 
             )
             return codes, scales
 
-        turned = psum.tile([P, P], F32, name="turned", tag="acc7")
-        nc.tensor.transpose(turned[:], bias_rows[:], ident[:])
-        nc.vector.tensor_copy(bias[:], turned[:, 0:M_TILES])
+        def quantise_x(i, copy):
+            n = pieces[i][1]
+            mix = held.tile([P, n, PACK], BF16, name="x_mix%d" % i, align_bytes=64)
+            copy(
+                mix[:].rearrange("p (c i) t -> p c t i", i=4),
+                x_raw[i][:].rearrange("p t (c i) -> p c t i", i=4),
+            )
+            return quantise(mix[:], n, "x%d" % i)
+
+        x_quant = [quantise_x(0, nc.scalar.copy)]
 
         s_mix = held.tile([P, S, PACK], BF16, name="s_mix", align_bytes=64)
-        for t in range(PACK - 1):
-            nc.vector.tensor_copy(s_mix[:, :, t], planes[t][:].indirect(offsets[:]))
-        mix0 = held.tile([P, 256, PACK], BF16, name="x_mix0", align_bytes=64)
-        nc.scalar.copy(mix0[:], x_raw[0][:].rearrange("p j n -> p n j"))
-        x0_quant = quantise(mix0[:], 256, "x0")
-        for h in range(2):
-            nc.vector.tensor_copy(
-                s_mix[:, h * HALF : (h + 1) * HALF, PACK - 1],
-                planes[PACK - 1][:].indirect(offsets[:, h * 16 : (h + 1) * 16]),
+        for t, window in enumerate((planes01[:, 0, :], planes01[:, 1, :], plane2[:])):
+            nc.vector.tensor_copy(s_mix[:, :, t], window.indirect(offsets[:]))
+
+        turned = psum.tile([P, P], F32, name="turned", tag="acc7")
+        nc.tensor.transpose(turned[:], bias_rows[:], ident[:])
+        bias = held.tile([P, M_TILES], F32, name="bias", tag="plane2", align_bytes=64)
+        nc.scalar.copy(bias[:], turned[:, 0:M_TILES])
+
+        warm = psum.tile([P, HALF], F32, name="warm", tag="acc7")
+        for i in range(4):
+            codes, plane = x_quant[0]
+            nc.tensor.matmul_mx(
+                out=warm[:],
+                lhsT=codes[:, 0:P].bitcast(FP8X4),
+                lhsT_scale=plane[:, 0:P],
+                rhs=codes[:].bitcast(FP8X4),
+                rhs_scale=plane[:],
+                start=i == 0,
+                stop=i == 3,
             )
-        s_quant = [quantise(s_mix[:, h * HALF : (h + 1) * HALF, :], HALF, "s%d" % h) for h in range(2)]
+
+        s_quant = []
+        for h, (lo, hi) in enumerate(((0, HALF + 32), (HALF, S))):
+            nc.vector.tensor_copy(
+                s_mix[:, lo:hi, PACK - 1],
+                plane3[:].indirect(offsets[:, lo // 16 : hi // 16]),
+            )
+            s_quant.append(quantise(s_mix[:, h * HALF : (h + 1) * HALF, :], HALF, "s%d" % h))
+        x_quant.append(quantise_x(1, nc.scalar.copy))
+        x_quant.append(quantise_x(2, nc.vector.tensor_copy))
+
+        def product(acc, words, scales, moving, lo, n, m, opens):
+            codes, plane = moving
+            nc.tensor.matmul_mx(
+                out=acc[:],
+                lhsT=words[:, m * P : (m + 1) * P].bitcast(FP8X4),
+                lhsT_scale=scales[:, m * P : (m + 1) * P],
+                rhs=codes[:, lo : lo + n].bitcast(FP8X4),
+                rhs_scale=plane[:, lo : lo + n],
+                start=opens,
+                stop=not opens,
+            )
 
         out_rows = out.rearrange("(m p) n -> p m n", p=P)
-
-        def products(accs, words, scales, moving, lo, n, opens):
-            codes, plane = moving
-            for m in range(M_TILES):
-                nc.tensor.matmul_mx(
-                    out=accs[m][:],
-                    lhsT=words[:, m * P : (m + 1) * P].bitcast(FP8X4),
-                    lhsT_scale=scales[:, m * P : (m + 1) * P],
-                    rhs=codes[:, lo : lo + n].bitcast(FP8X4),
-                    rhs_scale=plane[:, lo : lo + n],
-                    start=opens,
-                    stop=not opens,
-                )
-
-        def banks(i):
-            n = pieces[i][1]
-            return [
-                psum.tile([P, n], F32, name="acc%d_%d" % (i, m), tag="acc%d" % ((i % 2) * M_TILES + m))
-                for m in range(M_TILES)
-            ]
-
-        def leave(i, accs):
-            c, n = pieces[i]
-            for m0 in range(0, M_TILES, 2):
-                result = held.tile([P, 2, n], F32, name="result%d_%d" % (i, m0))
-                for m in (m0, m0 + 1):
-                    nc.scalar.activation(result[:, m - m0, :], accs[m][:], GELU, bias=bias[:, m : m + 1])
-                nc.sync.dma_start(out_rows[:, m0 : m0 + 2, c : c + n], result[:])
-
-        accs = banks(0)
-        products(accs, words1, scales1, x0_quant, 0, 256, True)
-        products(accs, words2, scales2, s_quant[0], 0, 256, False)
-        leave(0, accs)
-        for i in (1, 2):
-            accs = banks(i)
-            products(accs, words2, scales2, s_quant[1], pieces[i][0] - HALF, P, True)
-            mix = held.tile([P, P, PACK], BF16, name="x_mix%d" % i, align_bytes=64)
-            nc.vector.tensor_copy(mix[:], x_raw[i][:].rearrange("p j n -> p n j"))
-            products(accs, words1, scales1, quantise(mix[:], P, "x%d" % i), 0, P, False)
-            leave(i, accs)
+        for i, (c, n) in enumerate(pieces):
+            per_store = HALF // n
+            sides = [(words1, scales1, x_quant[i], 0), (words2, scales2, s_quant[c // HALF], c % HALF)]
+            first = 1 if i == 2 else 0
+            for m0 in range(0, M_TILES, per_store):
+                result = held.tile([P, per_store, n], F32, name="result%d_%d" % (i, m0))
+                for m in range(m0, m0 + per_store):
+                    acc = psum.tile([P, n], F32, name="acc%d_%d" % (i, m), tag="acc%d" % (i % 2 * M_TILES + m))
+                    product(acc, *sides[first], n, m, True)
+                    product(acc, *sides[1 - first], n, m, False)
+                    nc.scalar.activation(result[:, m - m0, :], acc[:], GELU, bias=bias[:, m : m + 1])
+                nc.sync.dma_start(out_rows[:, m0 : m0 + per_store, c : c + n], result[:])

@@ -30,11 +30,12 @@ def tile_picked_recall_gelu_e_kernel(tc, xT, sT, w1_words, w1_scales, w2_words, 
         psum = ctx.enter_context(tc.psum_pool(name="psum", bufs=1))
 
         offsets = held.tile([P, S // 16], U16, name="offsets")
-        planes01 = held.tile([P, 2, T], F32, name="planes01", align_bytes=64)
+        plane0 = held.tile([P, T], F32, name="plane0", align_bytes=64)
+        plane1 = held.tile([P, T], F32, name="plane1", align_bytes=64)
         plane2 = held.tile([P, T], F32, name="plane2", tag="plane2", align_bytes=64)
         plane3 = held.tile([P, T], F32, name="plane3", align_bytes=64)
         words1 = held.tile([P, N], I32, name="words1", align_bytes=64)
-        words2 = held.tile([P, N], I32, name="words2", align_bytes=64)
+        words2 = [held.tile([P, HALF], I32, name="words2_%d" % i, align_bytes=64) for i in range(2)]
         w_scales = held.tile([P, 2 * N], U8, name="w_scales", align_bytes=64)
         scales1 = w_scales[:, 0:N]
         scales2 = w_scales[:, N : 2 * N]
@@ -63,21 +64,23 @@ def tile_picked_recall_gelu_e_kernel(tc, xT, sT, w1_words, w1_scales, w2_words, 
             c, n = pieces[i]
             nc.sync.dma_start(x_raw[i][:], x_rows[:, :, c : c + n])
 
-        def load_words(words, source):
-            nc.sync.dma_start(words[:], source[0].rearrange("p m r -> p (m r)").bitcast(I32))
+        w1_rows = w1_words[0].rearrange("p m r -> p (m r)").bitcast(I32)
+        w2_rows = w2_words[0].rearrange("p m r -> p (m r)").bitcast(I32)
 
         nc.scalar.activation(dummy[:, 1:2], dummy[:, 0:1], GELU)
-        nc.sync.dma_start(planes01[:], s_rows[:, 0:2, :])
+        nc.sync.dma_start(plane0[:], s_rows[:, 0, :])
         nc.sync.dma_start(offsets[:], offs)
+        nc.sync.dma_start(plane1[:], s_rows[:, 1, :])
         load_scale_rows(scales1, w1_scales)
         load_x(0)
         nc.sync.dma_start(plane2[:], s_rows[:, 2, :])
         nc.sync.dma_start(bias_rows[0:M_TILES, :], b.rearrange("(m p) o -> m (p o)", p=P))
         load_scale_rows(scales2, w2_scales)
         nc.sync.dma_start(plane3[:], s_rows[:, 3, :])
-        load_words(words1, w1_words)
+        nc.sync.dma_start(words1[:], w1_rows)
         load_x(1)
-        load_words(words2, w2_words)
+        nc.sync.dma_start(words2[0][:], w2_rows[:, 0:HALF])
+        nc.sync.dma_start(words2[1][:], w2_rows[:, HALF:N])
         load_x(2)
 
         def quantise(mix, n, name):
@@ -100,7 +103,7 @@ def tile_picked_recall_gelu_e_kernel(tc, xT, sT, w1_words, w1_scales, w2_words, 
         x_quant = [quantise_x(0, nc.scalar.copy)]
 
         s_mix = held.tile([P, S, PACK], BF16, name="s_mix", align_bytes=64)
-        for t, window in enumerate((planes01[:, 0, :], planes01[:, 1, :], plane2[:])):
+        for t, window in enumerate((plane0[:], plane1[:], plane2[:])):
             nc.vector.tensor_copy(s_mix[:, :, t], window.indirect(offsets[:]))
 
         turned = psum.tile([P, P], F32, name="turned", tag="acc7")
@@ -121,13 +124,12 @@ def tile_picked_recall_gelu_e_kernel(tc, xT, sT, w1_words, w1_scales, w2_words, 
                 stop=i == 3,
             )
 
-        s_quant = []
-        for h, (lo, hi) in enumerate(((0, HALF + 32), (HALF, S))):
-            nc.vector.tensor_copy(
-                s_mix[:, lo:hi, PACK - 1],
-                plane3[:].indirect(offsets[:, lo // 16 : hi // 16]),
-            )
-            s_quant.append(quantise(s_mix[:, h * HALF : (h + 1) * HALF, :], HALF, "s%d" % h))
+        nc.vector.tensor_copy(s_mix[:, 0:HALF, PACK - 1], plane3[:].indirect(offsets[:, 0:16]))
+        s_quant = [quantise(s_mix[:, 0:HALF, :], HALF, "s0")]
+        picked = held.tile([P, HALF], BF16, name="picked", align_bytes=64)
+        nc.vector.tensor_copy(picked[:], plane3[:].indirect(offsets[:, 16:32]))
+        nc.vector.tensor_copy(s_mix[:, HALF:S, PACK - 1], picked[:])
+        s_quant.append(quantise(s_mix[:, HALF:S, :], HALF, "s1"))
         x_quant.append(quantise_x(1, nc.scalar.copy))
         x_quant.append(quantise_x(2, nc.vector.tensor_copy))
 
@@ -135,7 +137,7 @@ def tile_picked_recall_gelu_e_kernel(tc, xT, sT, w1_words, w1_scales, w2_words, 
             codes, plane = moving
             nc.tensor.matmul_mx(
                 out=acc[:],
-                lhsT=words[:, m * P : (m + 1) * P].bitcast(FP8X4),
+                lhsT=words[m].bitcast(FP8X4),
                 lhsT_scale=scales[:, m * P : (m + 1) * P],
                 rhs=codes[:, lo : lo + n].bitcast(FP8X4),
                 rhs_scale=plane[:, lo : lo + n],
@@ -143,15 +145,17 @@ def tile_picked_recall_gelu_e_kernel(tc, xT, sT, w1_words, w1_scales, w2_words, 
                 stop=not opens,
             )
 
+        w1_tiles = [words1[:, m * P : (m + 1) * P] for m in range(M_TILES)]
+        w2_tiles = [words2[m // 2][:, m % 2 * P : (m % 2 + 1) * P] for m in range(M_TILES)]
         out_rows = out.rearrange("(m p) n -> p m n", p=P)
         for i, (c, n) in enumerate(pieces):
             per_store = HALF // n
-            sides = [(words1, scales1, x_quant[i], 0), (words2, scales2, s_quant[c // HALF], c % HALF)]
-            first = 1 if i == 2 else 0
+            sides = [(w1_tiles, scales1, x_quant[i], 0), (w2_tiles, scales2, s_quant[c // HALF], c % HALF)]
             for m0 in range(0, M_TILES, per_store):
                 result = held.tile([P, per_store, n], F32, name="result%d_%d" % (i, m0))
                 for m in range(m0, m0 + per_store):
-                    acc = psum.tile([P, n], F32, name="acc%d_%d" % (i, m), tag="acc%d" % (i % 2 * M_TILES + m))
+                    acc = psum.tile([P, n], F32, name="acc%d_%d" % (i, m), tag="acc%d" % (i // 2 * M_TILES + m))
+                    first = 1 if i == 1 or (i == 2 and m >= 2) else 0
                     product(acc, *sides[first], n, m, True)
                     product(acc, *sides[1 - first], n, m, False)
                     nc.scalar.activation(result[:, m - m0, :], acc[:], GELU, bias=bias[:, m : m + 1])

@@ -32,7 +32,7 @@ def tile_picked_recall_gelu_e_kernel(tc, xT, sT, w1_words, w1_scales, w2_words, 
         offsets = held.tile([P, S // 16], U16, name="offsets")
         plane0 = held.tile([P, T], F32, name="plane0", align_bytes=64)
         plane1 = held.tile([P, T], F32, name="plane1", align_bytes=64)
-        plane2 = held.tile([P, T], F32, name="plane2", tag="plane2", align_bytes=64)
+        plane2 = held.tile([P, T], F32, name="plane2", align_bytes=64)
         plane3 = held.tile([P, T], F32, name="plane3", align_bytes=64)
         words1 = held.tile([P, N], I32, name="words1", align_bytes=64)
         words2 = [held.tile([P, HALF], I32, name="words2_%d" % i, align_bytes=64) for i in range(2)]
@@ -53,8 +53,8 @@ def tile_picked_recall_gelu_e_kernel(tc, xT, sT, w1_words, w1_scales, w2_words, 
         nc.vector.memset(dummy[:], 0.0)
         make_identity(nc, ident[:])
 
-        def load_scale_rows(scales, source):
-            for q in range(4):
+        def load_scale_rows(scales, source, quadrants):
+            for q in quadrants:
                 nc.sync.dma_start(
                     scales[32 * q : 32 * q + 4, :].bitcast(I32),
                     source[0, 4 * q : 4 * q + 4, :].bitcast(I32),
@@ -71,14 +71,15 @@ def tile_picked_recall_gelu_e_kernel(tc, xT, sT, w1_words, w1_scales, w2_words, 
         nc.sync.dma_start(plane0[:], s_rows[:, 0, :])
         nc.sync.dma_start(offsets[:], offs)
         nc.sync.dma_start(plane1[:], s_rows[:, 1, :])
-        load_scale_rows(scales1, w1_scales)
+        load_scale_rows(scales1, w1_scales, range(4))
         load_x(0)
         nc.sync.dma_start(plane2[:], s_rows[:, 2, :])
         nc.sync.dma_start(bias_rows[0:M_TILES, :], b.rearrange("(m p) o -> m (p o)", p=P))
-        load_scale_rows(scales2, w2_scales)
+        load_scale_rows(scales2, w2_scales, range(1))
         nc.sync.dma_start(plane3[:], s_rows[:, 3, :])
         nc.sync.dma_start(words1[:], w1_rows)
         load_x(1)
+        load_scale_rows(scales2, w2_scales, range(1, 4))
         nc.sync.dma_start(words2[0][:], w2_rows[:, 0:HALF])
         nc.sync.dma_start(words2[1][:], w2_rows[:, HALF:N])
         load_x(2)
@@ -103,26 +104,16 @@ def tile_picked_recall_gelu_e_kernel(tc, xT, sT, w1_words, w1_scales, w2_words, 
         x_quant = [quantise_x(0, nc.scalar.copy)]
 
         s_mix = held.tile([P, S, PACK], BF16, name="s_mix", align_bytes=64)
-        for t, window in enumerate((plane0[:], plane1[:], plane2[:])):
+        for t, window in enumerate((plane0[:], plane1[:])):
             nc.vector.tensor_copy(s_mix[:, :, t], window.indirect(offsets[:]))
+        picked2 = held.tile([P, S], BF16, name="picked2", align_bytes=64)
+        nc.vector.tensor_copy(picked2[:], plane2[:].indirect(offsets[:]))
+        nc.vector.tensor_copy(s_mix[:, :, 2], picked2[:])
 
         turned = psum.tile([P, P], F32, name="turned", tag="acc7")
         nc.tensor.transpose(turned[:], bias_rows[:], ident[:])
-        bias = held.tile([P, M_TILES], F32, name="bias", tag="plane2", align_bytes=64)
+        bias = held.tile([P, M_TILES], F32, name="bias")
         nc.scalar.copy(bias[:], turned[:, 0:M_TILES])
-
-        warm = psum.tile([P, HALF], F32, name="warm", tag="acc7")
-        for i in range(4):
-            codes, plane = x_quant[0]
-            nc.tensor.matmul_mx(
-                out=warm[:],
-                lhsT=codes[:, 0:P].bitcast(FP8X4),
-                lhsT_scale=plane[:, 0:P],
-                rhs=codes[:].bitcast(FP8X4),
-                rhs_scale=plane[:],
-                start=i == 0,
-                stop=i == 3,
-            )
 
         nc.vector.tensor_copy(s_mix[:, 0:HALF, PACK - 1], plane3[:].indirect(offsets[:, 0:16]))
         s_quant = [quantise(s_mix[:, 0:HALF, :], HALF, "s0")]

@@ -71,16 +71,16 @@ def tile_picked_recall_gelu_e_kernel(tc, xT, sT, w1_words, w1_scales, w2_words, 
         nc.sync.dma_start(plane0[:], s_rows[:, 0, :])
         nc.sync.dma_start(offsets[:], offs)
         nc.sync.dma_start(plane1[:], s_rows[:, 1, :])
-        load_scale_rows(scales1, w1_scales, range(4))
         load_x(0)
         nc.sync.dma_start(plane2[:], s_rows[:, 2, :])
         nc.sync.dma_start(bias_rows[0:M_TILES, :], b.rearrange("(m p) o -> m (p o)", p=P))
         load_scale_rows(scales2, w2_scales, range(1))
         nc.sync.dma_start(plane3[:], s_rows[:, 3, :])
+        load_scale_rows(scales1, w1_scales, range(4))
         nc.sync.dma_start(words1[:], w1_rows)
         load_x(1)
-        load_scale_rows(scales2, w2_scales, range(1, 4))
         nc.sync.dma_start(words2[0][:], w2_rows[:, 0:HALF])
+        load_scale_rows(scales2, w2_scales, range(1, 4))
         nc.sync.dma_start(words2[1][:], w2_rows[:, HALF:N])
         load_x(2)
 

@@ -11,7 +11,12 @@ N = 512
 PACK = 4
 HALF = 256
 M_TILES = N // P
+QUADRANTS = 4
+ENTRIES = 16
+LINE = 4
 FLOPS = 2 * 2 * K * N * S
+
+PIECES = ((0, 256), (256, 128), (384, 128))
 
 F32 = mybir.dt.float32
 BF16 = mybir.dt.bfloat16
@@ -29,11 +34,8 @@ def tile_picked_recall_gelu_e_kernel(tc, xT, sT, w1_words, w1_scales, w2_words, 
         held = ctx.enter_context(tc.tile_pool(name="held", bufs=1))
         psum = ctx.enter_context(tc.psum_pool(name="psum", bufs=1))
 
-        offsets = held.tile([P, S // 16], U16, name="offsets")
-        plane0 = held.tile([P, T], F32, name="plane0", align_bytes=64)
-        plane1 = held.tile([P, T], F32, name="plane1", align_bytes=64)
-        plane2 = held.tile([P, T], F32, name="plane2", align_bytes=64)
-        plane3 = held.tile([P, T], F32, name="plane3", align_bytes=64)
+        offsets = held.tile([P, S // ENTRIES], U16, name="offsets")
+        planes = [held.tile([P, T], F32, name="plane%d" % t, align_bytes=64) for t in range(PACK)]
         words1 = held.tile([P, N], I32, name="words1", align_bytes=64)
         words2 = [held.tile([P, HALF], I32, name="words2_%d" % i, align_bytes=64) for i in range(2)]
         w_scales = held.tile([P, 2 * N], U8, name="w_scales", align_bytes=64)
@@ -42,11 +44,10 @@ def tile_picked_recall_gelu_e_kernel(tc, xT, sT, w1_words, w1_scales, w2_words, 
         bias_rows = held.tile([P, P], F32, name="bias_rows")
         ident = held.tile([P, P], F32, name="ident")
         dummy = held.tile([P, 2], F32, name="dummy")
-        pieces = ((0, 256), (256, 128), (384, 128))
-        x_raw = [held.tile([P, PACK, n], F32, name="x_raw%d" % c, align_bytes=64) for c, n in pieces]
+        x_raw = [held.tile([P, PACK, n], F32, name="x_raw%d" % c, align_bytes=64) for c, n in PIECES]
 
         s_rows = sT.rearrange("(p t) c -> p t c", t=PACK)
-        x_rows = xT.rearrange("(p j) n -> p j n", j=PACK)
+        x_rows = xT.rearrange("(p t) n -> p t n", t=PACK)
 
         nc.gpsimd.memset(w_scales[:].bitcast(I32), 0)
         nc.gpsimd.memset(bias_rows[:], 0.0)
@@ -61,26 +62,27 @@ def tile_picked_recall_gelu_e_kernel(tc, xT, sT, w1_words, w1_scales, w2_words, 
                 )
 
         def load_x(i):
-            c, n = pieces[i]
+            c, n = PIECES[i]
             nc.sync.dma_start(x_raw[i][:], x_rows[:, :, c : c + n])
 
         w1_rows = w1_words[0].rearrange("p m r -> p (m r)").bitcast(I32)
         w2_rows = w2_words[0].rearrange("p m r -> p (m r)").bitcast(I32)
 
         nc.scalar.activation(dummy[:, 1:2], dummy[:, 0:1], GELU)
-        nc.sync.dma_start(plane0[:], s_rows[:, 0, :])
+
+        nc.sync.dma_start(planes[0][:], s_rows[:, 0, :])
         nc.sync.dma_start(offsets[:], offs)
-        nc.sync.dma_start(plane1[:], s_rows[:, 1, :])
+        nc.sync.dma_start(planes[1][:], s_rows[:, 1, :])
         load_x(0)
-        nc.sync.dma_start(plane2[:], s_rows[:, 2, :])
+        nc.sync.dma_start(planes[2][:], s_rows[:, 2, :])
         nc.sync.dma_start(bias_rows[0:M_TILES, :], b.rearrange("(m p) o -> m (p o)", p=P))
         load_scale_rows(scales2, w2_scales, range(1))
-        nc.sync.dma_start(plane3[:], s_rows[:, 3, :])
-        load_scale_rows(scales1, w1_scales, range(4))
+        nc.sync.dma_start(planes[3][:], s_rows[:, 3, :])
+        load_scale_rows(scales1, w1_scales, range(QUADRANTS))
         nc.sync.dma_start(words1[:], w1_rows)
         load_x(1)
         nc.sync.dma_start(words2[0][:], w2_rows[:, 0:HALF])
-        load_scale_rows(scales2, w2_scales, range(1, 4))
+        load_scale_rows(scales2, w2_scales, range(1, QUADRANTS))
         nc.sync.dma_start(words2[1][:], w2_rows[:, HALF:N])
         load_x(2)
 
@@ -92,22 +94,22 @@ def tile_picked_recall_gelu_e_kernel(tc, xT, sT, w1_words, w1_scales, w2_words, 
             )
             return codes, scales
 
-        def quantise_x(i, copy):
-            n = pieces[i][1]
+        def interleave(copy, mix, raw):
+            copy(mix.rearrange("p (c i) t -> p c t i", i=LINE), raw.rearrange("p t (c i) -> p c t i", i=LINE))
+
+        def quantise_on_scalar(i):
+            n = PIECES[i][1]
             mix = held.tile([P, n, PACK], BF16, name="x_mix%d" % i, align_bytes=64)
-            copy(
-                mix[:].rearrange("p (c i) t -> p c t i", i=4),
-                x_raw[i][:].rearrange("p t (c i) -> p c t i", i=4),
-            )
+            interleave(nc.scalar.copy, mix[:], x_raw[i][:])
             return quantise(mix[:], n, "x%d" % i)
 
-        x_quant = [quantise_x(0, nc.scalar.copy)]
+        x_quant = [quantise_on_scalar(0)]
 
         s_mix = held.tile([P, S, PACK], BF16, name="s_mix", align_bytes=64)
-        for t, window in enumerate((plane0[:], plane1[:])):
-            nc.vector.tensor_copy(s_mix[:, :, t], window.indirect(offsets[:]))
+        for t in range(2):
+            nc.vector.tensor_copy(s_mix[:, :, t], planes[t][:].indirect(offsets[:]))
         picked2 = held.tile([P, S], BF16, name="picked2", align_bytes=64)
-        nc.vector.tensor_copy(picked2[:], plane2[:].indirect(offsets[:]))
+        nc.vector.tensor_copy(picked2[:], planes[2][:].indirect(offsets[:]))
         nc.vector.tensor_copy(s_mix[:, :, 2], picked2[:])
 
         turned = psum.tile([P, P], F32, name="turned", tag="acc7")
@@ -115,39 +117,61 @@ def tile_picked_recall_gelu_e_kernel(tc, xT, sT, w1_words, w1_scales, w2_words, 
         bias = held.tile([P, M_TILES], F32, name="bias")
         nc.scalar.copy(bias[:], turned[:, 0:M_TILES])
 
-        nc.vector.tensor_copy(s_mix[:, 0:HALF, PACK - 1], plane3[:].indirect(offsets[:, 0:16]))
+        half_columns = HALF // ENTRIES
+        nc.vector.tensor_copy(s_mix[:, 0:HALF, 3], planes[3][:].indirect(offsets[:, 0:half_columns]))
         s_quant = [quantise(s_mix[:, 0:HALF, :], HALF, "s0")]
-        picked = held.tile([P, HALF], BF16, name="picked", align_bytes=64)
-        nc.vector.tensor_copy(picked[:], plane3[:].indirect(offsets[:, 16:32]))
-        nc.vector.tensor_copy(s_mix[:, HALF:S, PACK - 1], picked[:])
+        picked3 = held.tile([P, HALF], BF16, name="picked", align_bytes=64)
+        nc.vector.tensor_copy(picked3[:], planes[3][:].indirect(offsets[:, half_columns : 2 * half_columns]))
+        nc.vector.tensor_copy(s_mix[:, HALF:S, 3], picked3[:])
         s_quant.append(quantise(s_mix[:, HALF:S, :], HALF, "s1"))
-        x_quant.append(quantise_x(1, nc.scalar.copy))
-        x_quant.append(quantise_x(2, nc.vector.tensor_copy))
 
-        def product(acc, words, scales, moving, lo, n, m, opens):
-            codes, plane = moving
+        x_quant.append(quantise_on_scalar(1))
+
+        x_mix2 = held.tile([P, P, PACK], BF16, name="x_mix2", align_bytes=64)
+        x2_codes = held.tile([P, P], U32, name="x2_codes", align_bytes=64)
+        x2_scales = held.tile([P, P], U8, name="x2_scales", align_bytes=64)
+        halves = (slice(0, P // 2), slice(P // 2, P))
+        for cols in halves:
+            interleave(nc.vector.tensor_copy, x_mix2[:, cols, :], x_raw[2][:, :, cols])
+        for cols in halves:
+            nc.vector.quantize_mx(
+                out=x2_codes[:, cols].bitcast(FP8X4),
+                scales=x2_scales[:, cols],
+                in_=x_mix2[:, cols, :].rearrange("p n t -> p (n t)"),
+            )
+        x_quant.append((x2_codes, x2_scales))
+
+        def product(acc, words, w_scale, moving, lo, n, m, opens):
+            codes, scales = moving
             nc.tensor.matmul_mx(
                 out=acc[:],
                 lhsT=words[m].bitcast(FP8X4),
-                lhsT_scale=scales[:, m * P : (m + 1) * P],
+                lhsT_scale=w_scale[:, m * P : (m + 1) * P],
                 rhs=codes[:, lo : lo + n].bitcast(FP8X4),
-                rhs_scale=plane[:, lo : lo + n],
+                rhs_scale=scales[:, lo : lo + n],
                 start=opens,
                 stop=not opens,
             )
 
         w1_tiles = [words1[:, m * P : (m + 1) * P] for m in range(M_TILES)]
         w2_tiles = [words2[m // 2][:, m % 2 * P : (m % 2 + 1) * P] for m in range(M_TILES)]
+
+        def bank(i, m):
+            if i == 0:
+                return m
+            return 2 * (i - 1) + m % 2 + M_TILES * (m // 2)
+
         out_rows = out.rearrange("(m p) n -> p m n", p=P)
-        for i, (c, n) in enumerate(pieces):
+        for i, (c, n) in enumerate(PIECES):
             per_store = HALF // n
-            sides = [(w1_tiles, scales1, x_quant[i], 0), (w2_tiles, scales2, s_quant[c // HALF], c % HALF)]
+            queries = (w1_tiles, scales1, x_quant[i], 0)
+            memories = (w2_tiles, scales2, s_quant[c // HALF], c % HALF)
             for m0 in range(0, M_TILES, per_store):
                 result = held.tile([P, per_store, n], F32, name="result%d_%d" % (i, m0))
                 for m in range(m0, m0 + per_store):
-                    acc = psum.tile([P, n], F32, name="acc%d_%d" % (i, m), tag="acc%d" % (i // 2 * M_TILES + m))
-                    first = 1 if i == 1 or (i == 2 and m >= 2) else 0
-                    product(acc, *sides[first], n, m, True)
-                    product(acc, *sides[1 - first], n, m, False)
+                    acc = psum.tile([P, n], F32, name="acc%d_%d" % (i, m), tag="acc%d" % bank(i, m))
+                    first, second = (queries, memories) if i == 0 else (memories, queries)
+                    product(acc, *first, n, m, True)
+                    product(acc, *second, n, m, False)
                     nc.scalar.activation(result[:, m - m0, :], acc[:], GELU, bias=bias[:, m : m + 1])
                 nc.sync.dma_start(out_rows[:, m0 : m0 + per_store, c : c + n], result[:])

@@ -103,7 +103,17 @@ def tile_picked_recall_gelu_e_kernel(tc, xT, sT, w1_words, w1_scales, w2_words, 
             interleave(nc.scalar.copy, mix[:], x_raw[i][:])
             return quantise(mix[:], n, "x%d" % i)
 
-        x_quant = [quantise_on_scalar(0)]
+        x_mix0 = held.tile([P, HALF, PACK], BF16, name="x_mix0", align_bytes=64)
+        interleave(nc.scalar.copy, x_mix0[:], x_raw[0][:])
+        x0_codes = held.tile([P, S], U32, name="x0_codes", align_bytes=64)
+        x0_scales = held.tile([P, S], U8, name="x0_scales", align_bytes=64)
+        for cols in (slice(0, HALF), slice(HALF, S)):
+            nc.vector.quantize_mx(
+                out=x0_codes[:, cols].bitcast(FP8X4),
+                scales=x0_scales[:, cols],
+                in_=x_mix0[:].rearrange("p n t -> p (n t)"),
+            )
+        x_quant = [(x0_codes, x0_scales)]
 
         s_mix = held.tile([P, S, PACK], BF16, name="s_mix", align_bytes=64)
         for t in range(2):
@@ -116,6 +126,18 @@ def tile_picked_recall_gelu_e_kernel(tc, xT, sT, w1_words, w1_scales, w2_words, 
         nc.tensor.transpose(turned[:], bias_rows[:], ident[:])
         bias = held.tile([P, M_TILES], F32, name="bias")
         nc.scalar.copy(bias[:], turned[:, 0:M_TILES])
+
+        unread = psum.tile([P, S], F32, name="unread", tag="acc7")
+        for i in range(2):
+            nc.tensor.matmul_mx(
+                out=unread[:],
+                lhsT=x0_codes[:, 0:P].bitcast(FP8X4),
+                lhsT_scale=x0_scales[:, 0:P],
+                rhs=x0_codes[:].bitcast(FP8X4),
+                rhs_scale=x0_scales[:],
+                start=True,
+                stop=True,
+            )
 
         half_columns = HALF // ENTRIES
         nc.vector.tensor_copy(s_mix[:, 0:HALF, 3], planes[3][:].indirect(offsets[:, 0:half_columns]))

@@ -73,16 +73,16 @@ def tile_picked_recall_gelu_e_kernel(tc, xT, sT, w1_words, w1_scales, w2_words, 
         nc.sync.dma_start(planes[0][:], s_rows[:, 0, :])
         nc.sync.dma_start(offsets[:], offs)
         nc.sync.dma_start(planes[1][:], s_rows[:, 1, :])
+        load_scale_rows(scales1, w1_scales, range(QUADRANTS))
         load_x(0)
         nc.sync.dma_start(planes[2][:], s_rows[:, 2, :])
         nc.sync.dma_start(bias_rows[0:M_TILES, :], b.rearrange("(m p) o -> m (p o)", p=P))
-        load_scale_rows(scales2, w2_scales, range(1))
+        load_scale_rows(scales2, w2_scales, range(2))
         nc.sync.dma_start(planes[3][:], s_rows[:, 3, :])
-        load_scale_rows(scales1, w1_scales, range(QUADRANTS))
+        load_scale_rows(scales2, w2_scales, range(2, QUADRANTS))
         nc.sync.dma_start(words1[:], w1_rows)
         load_x(1)
         nc.sync.dma_start(words2[0][:], w2_rows[:, 0:HALF])
-        load_scale_rows(scales2, w2_scales, range(1, QUADRANTS))
         nc.sync.dma_start(words2[1][:], w2_rows[:, HALF:N])
         load_x(2)
 
@@ -119,8 +119,15 @@ def tile_picked_recall_gelu_e_kernel(tc, xT, sT, w1_words, w1_scales, w2_words, 
         for t in range(2):
             nc.vector.tensor_copy(s_mix[:, :, t], planes[t][:].indirect(offsets[:]))
         picked2 = held.tile([P, S], BF16, name="picked2", align_bytes=64)
-        nc.vector.tensor_copy(picked2[:], planes[2][:].indirect(offsets[:]))
-        nc.vector.tensor_copy(s_mix[:, :, 2], picked2[:])
+        half_columns = HALF // ENTRIES
+        for h in range(2):
+            cols = slice(h * HALF, (h + 1) * HALF)
+            nc.vector.tensor_copy(
+                picked2[:, cols], planes[2][:].indirect(offsets[:, h * half_columns : (h + 1) * half_columns])
+            )
+        for h in range(2):
+            cols = slice(h * HALF, (h + 1) * HALF)
+            nc.vector.tensor_copy(s_mix[:, cols, 2], picked2[:, cols])
 
         turned = psum.tile([P, P], F32, name="turned", tag="acc7")
         nc.tensor.transpose(turned[:], bias_rows[:], ident[:])
@@ -139,7 +146,6 @@ def tile_picked_recall_gelu_e_kernel(tc, xT, sT, w1_words, w1_scales, w2_words, 
                 stop=True,
             )
 
-        half_columns = HALF // ENTRIES
         nc.vector.tensor_copy(s_mix[:, 0:HALF, 3], planes[3][:].indirect(offsets[:, 0:half_columns]))
         s_quant = [quantise(s_mix[:, 0:HALF, :], HALF, "s0")]
         picked3 = held.tile([P, HALF], BF16, name="picked", align_bytes=64)
@@ -178,22 +184,21 @@ def tile_picked_recall_gelu_e_kernel(tc, xT, sT, w1_words, w1_scales, w2_words, 
         w1_tiles = [words1[:, m * P : (m + 1) * P] for m in range(M_TILES)]
         w2_tiles = [words2[m // 2][:, m % 2 * P : (m % 2 + 1) * P] for m in range(M_TILES)]
 
-        def bank(i, m):
-            if i == 0:
-                return m
-            return 2 * (i - 1) + m % 2 + M_TILES * (m // 2)
-
         out_rows = out.rearrange("(m p) n -> p m n", p=P)
-        for i, (c, n) in enumerate(PIECES):
-            per_store = HALF // n
-            queries = (w1_tiles, scales1, x_quant[i], 0)
+        units = [(0, 0, P, 0), (0, P, P, 1), (1, 0, HALF, 2), (2, 0, HALF, 3), (3, 0, HALF, 4)]
+        units += [(m, HALF, P, (0, 1, 5, 6)[m]) for m in range(M_TILES)]
+        units += [(m, HALF + P, P, (2, 3, 7, 4)[m]) for m in range(M_TILES)]
+        result = held.tile([P, M_TILES, S], F32, name="result")
+        for m, c, n, bank in units:
+            piece = 0 if c < HALF else c // P - 1
+            queries = (w1_tiles, scales1, x_quant[piece], c - PIECES[piece][0])
             memories = (w2_tiles, scales2, s_quant[c // HALF], c % HALF)
-            for m0 in range(0, M_TILES, per_store):
-                result = held.tile([P, per_store, n], F32, name="result%d_%d" % (i, m0))
-                for m in range(m0, m0 + per_store):
-                    acc = psum.tile([P, n], F32, name="acc%d_%d" % (i, m), tag="acc%d" % bank(i, m))
-                    first, second = (queries, memories) if i == 0 else (memories, queries)
-                    product(acc, *first, n, m, True)
-                    product(acc, *second, n, m, False)
-                    nc.scalar.activation(result[:, m - m0, :], acc[:], GELU, bias=bias[:, m : m + 1])
-                nc.sync.dma_start(out_rows[:, m0 : m0 + per_store, c : c + n], result[:])
+            acc = psum.tile([P, n], F32, name="acc%d_%d" % (m, c), tag="acc%d" % bank)
+            first, second = (queries, memories) if piece == 0 else (memories, queries)
+            product(acc, *first, n, m, True)
+            product(acc, *second, n, m, False)
+            nc.scalar.activation(result[:, m, c : c + n], acc[:], GELU, bias=bias[:, m : m + 1])
+            if piece == 0:
+                nc.sync.dma_start(out_rows[:, m, c : c + n], result[:, m, c : c + n])
+            elif m % 2 == 1:
+                nc.sync.dma_start(out_rows[:, m - 1 : m + 1, c : c + n], result[:, m - 1 : m + 1, c : c + n])

@@ -77,9 +77,8 @@ def tile_picked_recall_gelu_e_kernel(tc, xT, sT, w1_words, w1_scales, w2_words, 
         load_x(0)
         nc.sync.dma_start(planes[2][:], s_rows[:, 2, :])
         nc.sync.dma_start(bias_rows[0:M_TILES, :], b.rearrange("(m p) o -> m (p o)", p=P))
-        load_scale_rows(scales2, w2_scales, range(2))
         nc.sync.dma_start(planes[3][:], s_rows[:, 3, :])
-        load_scale_rows(scales2, w2_scales, range(2, QUADRANTS))
+        load_scale_rows(scales2, w2_scales, range(QUADRANTS))
         nc.sync.dma_start(words1[:], w1_rows)
         load_x(1)
         nc.sync.dma_start(words2[0][:], w2_rows[:, 0:HALF])

@@ -38,9 +38,9 @@ def tile_picked_recall_gelu_e_kernel(tc, xT, sT, w1_words, w1_scales, w2_words, 
         planes = [held.tile([P, T], F32, name="plane%d" % t, align_bytes=64) for t in range(PACK)]
         words1 = held.tile([P, N], I32, name="words1", align_bytes=64)
         words2 = [held.tile([P, HALF], I32, name="words2_%d" % i, align_bytes=64) for i in range(2)]
-        w_scales = held.tile([P, 2 * N], U8, name="w_scales", align_bytes=64)
-        scales1 = w_scales[:, 0:N]
-        scales2 = w_scales[:, N : 2 * N]
+        w_scales = held.tile([P, N], U8, name="w_scales", align_bytes=64)
+        scales1 = w_scales[:, :]
+        scales2 = w_scales[PACK:P, :]
         bias_rows = held.tile([P, P], F32, name="bias_rows")
         ident = held.tile([P, P], F32, name="ident")
         dummy = held.tile([P, 2], F32, name="dummy")
@@ -54,12 +54,9 @@ def tile_picked_recall_gelu_e_kernel(tc, xT, sT, w1_words, w1_scales, w2_words, 
         nc.vector.memset(dummy[:], 0.0)
         make_identity(nc, ident[:])
 
-        def load_scale_rows(scales, source, quadrants):
-            for q in quadrants:
-                nc.sync.dma_start(
-                    scales[32 * q : 32 * q + 4, :].bitcast(I32),
-                    source[0, 4 * q : 4 * q + 4, :].bitcast(I32),
-                )
+        def load_scale_rows(first, source):
+            for r in range(PACK):
+                nc.sync.dma_start(w_scales[first + r : P : 32, :].bitcast(I32), source[0, r:16:PACK, :].bitcast(I32))
 
         def load_x(i):
             c, n = PIECES[i]
@@ -73,12 +70,12 @@ def tile_picked_recall_gelu_e_kernel(tc, xT, sT, w1_words, w1_scales, w2_words, 
         nc.sync.dma_start(planes[0][:], s_rows[:, 0, :])
         nc.sync.dma_start(offsets[:], offs)
         nc.sync.dma_start(planes[1][:], s_rows[:, 1, :])
-        load_scale_rows(scales1, w1_scales, range(QUADRANTS))
+        load_scale_rows(0, w1_scales)
         load_x(0)
         nc.sync.dma_start(planes[2][:], s_rows[:, 2, :])
-        nc.sync.dma_start(bias_rows[0:M_TILES, :], b.rearrange("(m p) o -> m (p o)", p=P))
+        nc.sync.dma_start(bias_rows[8:P:32, :], b.rearrange("(m p) o -> m (p o)", p=P))
         nc.sync.dma_start(planes[3][:], s_rows[:, 3, :])
-        load_scale_rows(scales2, w2_scales, range(QUADRANTS))
+        load_scale_rows(PACK, w2_scales)
         nc.sync.dma_start(words1[:], w1_rows)
         load_x(1)
         nc.sync.dma_start(words2[0][:], w2_rows[:, 0:HALF])
@@ -131,7 +128,7 @@ def tile_picked_recall_gelu_e_kernel(tc, xT, sT, w1_words, w1_scales, w2_words, 
         turned = psum.tile([P, P], F32, name="turned", tag="acc7")
         nc.tensor.transpose(turned[:], bias_rows[:], ident[:])
         bias = held.tile([P, M_TILES], F32, name="bias")
-        nc.scalar.copy(bias[:], turned[:, 0:M_TILES])
+        nc.scalar.copy(bias[:], turned[:, 8:P:32])
 
         unread = psum.tile([P, S], F32, name="unread", tag="acc7")
         for i in range(2):

@@ -93,12 +93,6 @@ def tile_picked_recall_gelu_e_kernel(tc, xT, sT, w1_words, w1_scales, w2_words, 
         def interleave(copy, mix, raw):
             copy(mix.rearrange("p (c i) t -> p c t i", i=LINE), raw.rearrange("p t (c i) -> p c t i", i=LINE))
 
-        def quantise_on_scalar(i):
-            n = PIECES[i][1]
-            mix = held.tile([P, n, PACK], BF16, name="x_mix%d" % i, align_bytes=64)
-            interleave(nc.scalar.copy, mix[:], x_raw[i][:])
-            return quantise(mix[:], n, "x%d" % i)
-
         x_mix0 = held.tile([P, HALF, PACK], BF16, name="x_mix0", align_bytes=64)
         interleave(nc.scalar.copy, x_mix0[:], x_raw[0][:])
         x0_codes = held.tile([P, S], U32, name="x0_codes", align_bytes=64)
@@ -114,16 +108,11 @@ def tile_picked_recall_gelu_e_kernel(tc, xT, sT, w1_words, w1_scales, w2_words, 
         s_mix = held.tile([P, S, PACK], BF16, name="s_mix", align_bytes=64)
         for t in range(2):
             nc.vector.tensor_copy(s_mix[:, :, t], planes[t][:].indirect(offsets[:]))
-        picked2 = held.tile([P, S], BF16, name="picked2", align_bytes=64)
+        picked2 = held.tile([P, HALF], BF16, name="picked2", align_bytes=64)
         half_columns = HALF // ENTRIES
-        for h in range(2):
-            cols = slice(h * HALF, (h + 1) * HALF)
-            nc.vector.tensor_copy(
-                picked2[:, cols], planes[2][:].indirect(offsets[:, h * half_columns : (h + 1) * half_columns])
-            )
-        for h in range(2):
-            cols = slice(h * HALF, (h + 1) * HALF)
-            nc.vector.tensor_copy(s_mix[:, cols, 2], picked2[:, cols])
+        nc.vector.tensor_copy(picked2[:], planes[2][:].indirect(offsets[:, half_columns : 2 * half_columns]))
+        nc.vector.tensor_copy(s_mix[:, 0:HALF, 2], planes[2][:].indirect(offsets[:, 0:half_columns]))
+        nc.vector.tensor_copy(s_mix[:, HALF:S, 2], picked2[:])
 
         turned = psum.tile([P, P], F32, name="turned", tag="acc7")
         nc.tensor.transpose(turned[:], bias_rows[:], ident[:])
@@ -142,28 +131,31 @@ def tile_picked_recall_gelu_e_kernel(tc, xT, sT, w1_words, w1_scales, w2_words, 
                 stop=True,
             )
 
-        nc.vector.tensor_copy(s_mix[:, 0:HALF, 3], planes[3][:].indirect(offsets[:, 0:half_columns]))
-        s_quant = [quantise(s_mix[:, 0:HALF, :], HALF, "s0")]
         picked3 = held.tile([P, HALF], BF16, name="picked", align_bytes=64)
         nc.vector.tensor_copy(picked3[:], planes[3][:].indirect(offsets[:, half_columns : 2 * half_columns]))
-        nc.vector.tensor_copy(s_mix[:, HALF:S, 3], picked3[:])
+        nc.scalar.copy(s_mix[:, HALF:S, 3], picked3[:])
+        nc.vector.tensor_copy(s_mix[:, 0:HALF, 3], planes[3][:].indirect(offsets[:, 0:half_columns]))
+        s_quant = [quantise(s_mix[:, 0:HALF, :], HALF, "s0")]
         s_quant.append(quantise(s_mix[:, HALF:S, :], HALF, "s1"))
 
-        x_quant.append(quantise_on_scalar(1))
+        late_mix = held.tile([P, HALF, PACK], BF16, name="late_mix", align_bytes=64)
+        late_codes = held.tile([P, HALF], U32, name="late_codes", align_bytes=64)
+        late_scales = held.tile([P, HALF], U8, name="late_scales", align_bytes=64)
 
-        x_mix2 = held.tile([P, P, PACK], BF16, name="x_mix2", align_bytes=64)
-        x2_codes = held.tile([P, P], U32, name="x2_codes", align_bytes=64)
-        x2_scales = held.tile([P, P], U8, name="x2_scales", align_bytes=64)
-        halves = (slice(0, P // 2), slice(P // 2, P))
-        for cols in halves:
-            interleave(nc.vector.tensor_copy, x_mix2[:, cols, :], x_raw[2][:, :, cols])
-        for cols in halves:
+        def quantise_late(lo, n):
             nc.vector.quantize_mx(
-                out=x2_codes[:, cols].bitcast(FP8X4),
-                scales=x2_scales[:, cols],
-                in_=x_mix2[:, cols, :].rearrange("p n t -> p (n t)"),
+                out=late_codes[:, lo : lo + n].bitcast(FP8X4),
+                scales=late_scales[:, lo : lo + n],
+                in_=late_mix[:, lo : lo + n, :].rearrange("p n t -> p (n t)"),
             )
-        x_quant.append((x2_codes, x2_scales))
+
+        interleave(nc.scalar.copy, late_mix[:, 0:P, :], x_raw[1][:])
+        quantise_late(0, P)
+        for lo in (0, P // 2):
+            interleave(nc.vector.tensor_copy, late_mix[:, P + lo : P + lo + P // 2, :], x_raw[2][:, :, lo : lo + P // 2])
+        for lo in (0, P // 2):
+            quantise_late(P + lo, P // 2)
+        x_quant.append((late_codes, late_scales))
 
         def product(acc, words, w_scale, moving, lo, n, m, opens):
             codes, scales = moving
@@ -181,20 +173,28 @@ def tile_picked_recall_gelu_e_kernel(tc, xT, sT, w1_words, w1_scales, w2_words, 
         w2_tiles = [words2[m // 2][:, m % 2 * P : (m % 2 + 1) * P] for m in range(M_TILES)]
 
         out_rows = out.rearrange("(m p) n -> p m n", p=P)
-        units = [(0, 0, P, 0), (0, P, P, 1), (1, 0, HALF, 2), (2, 0, HALF, 3), (3, 0, HALF, 4)]
-        units += [(m, HALF, P, (0, 1, 5, 6)[m]) for m in range(M_TILES)]
-        units += [(m, HALF + P, P, (2, 3, 7, 4)[m]) for m in range(M_TILES)]
         result = held.tile([P, M_TILES, S], F32, name="result")
-        for m, c, n, bank in units:
-            piece = 0 if c < HALF else c // P - 1
-            queries = (w1_tiles, scales1, x_quant[piece], c - PIECES[piece][0])
-            memories = (w2_tiles, scales2, s_quant[c // HALF], c % HALF)
+
+        def step(m, c, n, bank):
+            half = c // HALF
+            queries = (w1_tiles, scales1, x_quant[half], c % HALF)
+            memories = (w2_tiles, scales2, s_quant[half], c % HALF)
             acc = psum.tile([P, n], F32, name="acc%d_%d" % (m, c), tag="acc%d" % bank)
-            first, second = (queries, memories) if piece == 0 else (memories, queries)
+            first, second = (queries, memories) if half == 0 else (memories, queries)
             product(acc, *first, n, m, True)
             product(acc, *second, n, m, False)
             nc.scalar.activation(result[:, m, c : c + n], acc[:], GELU, bias=bias[:, m : m + 1])
-            if piece == 0:
-                nc.sync.dma_start(out_rows[:, m, c : c + n], result[:, m, c : c + n])
-            elif m % 2 == 1:
-                nc.sync.dma_start(out_rows[:, m - 1 : m + 1, c : c + n], result[:, m - 1 : m + 1, c : c + n])
+
+        def store(first, last, c, n):
+            nc.sync.dma_start(out_rows[:, first : last + 1, c : c + n], result[:, first : last + 1, c : c + n])
+
+        for bank, (m, c, n) in enumerate(((0, 0, P), (0, P, P), (1, 0, HALF), (2, 0, HALF), (3, 0, HALF))):
+            step(m, c, n, bank)
+            store(m, m, c, n)
+        for c, banks in ((HALF, (5, 6)), (HALF + P, (7, 0))):
+            step(2, c, P, banks[0])
+            step(3, c, P, banks[1])
+            store(2, 3, c, P)
+        for m in range(2):
+            step(m, HALF, HALF, 1 + m)
+            store(m, m, HALF, HALF)

@@ -11,7 +11,6 @@ N = 512
 PACK = 4
 HALF = 256
 M_TILES = N // P
-QUADRANTS = 4
 ENTRIES = 16
 LINE = 4
 FLOPS = 2 * 2 * K * N * S
@@ -26,6 +25,7 @@ U16 = mybir.dt.uint16
 U8 = mybir.dt.uint8
 FP8X4 = mybir.dt.float8_e4m3fn_x4
 GELU = mybir.ActivationFunctionType.Gelu_apprx_tanh
+COPY = mybir.ActivationFunctionType.Copy
 
 
 def tile_picked_recall_gelu_e_kernel(tc, xT, sT, w1_words, w1_scales, w2_words, w2_scales, b, offs, out):
@@ -48,6 +48,8 @@ def tile_picked_recall_gelu_e_kernel(tc, xT, sT, w1_words, w1_scales, w2_words, 
 
         s_rows = sT.rearrange("(p t) c -> p t c", t=PACK)
         x_rows = xT.rearrange("(p t) n -> p t n", t=PACK)
+        w1_rows = w1_words[0].rearrange("p m r -> p (m r)").bitcast(I32)
+        w2_rows = w2_words[0].rearrange("p m r -> p (m r)").bitcast(I32)
 
         nc.gpsimd.memset(w_scales[:].bitcast(I32), 0)
         nc.gpsimd.memset(bias_rows[:], 0.0)
@@ -62,9 +64,6 @@ def tile_picked_recall_gelu_e_kernel(tc, xT, sT, w1_words, w1_scales, w2_words, 
             c, n = PIECES[i]
             nc.sync.dma_start(x_raw[i][:], x_rows[:, :, c : c + n])
 
-        w1_rows = w1_words[0].rearrange("p m r -> p (m r)").bitcast(I32)
-        w2_rows = w2_words[0].rearrange("p m r -> p (m r)").bitcast(I32)
-
         nc.scalar.activation(dummy[:, 1:2], dummy[:, 0:1], GELU)
 
         nc.sync.dma_start(planes[0][:], s_rows[:, 0, :])
@@ -77,18 +76,13 @@ def tile_picked_recall_gelu_e_kernel(tc, xT, sT, w1_words, w1_scales, w2_words, 
         nc.sync.dma_start(planes[3][:], s_rows[:, 3, :])
         load_scale_rows(PACK, w2_scales)
         nc.sync.dma_start(words1[:], w1_rows)
-        load_x(1)
         nc.sync.dma_start(words2[0][:], w2_rows[:, 0:HALF])
+        load_x(1)
         nc.sync.dma_start(words2[1][:], w2_rows[:, HALF:N])
         load_x(2)
 
-        def quantise(mix, n, name):
-            codes = held.tile([P, n], U32, name=name + "_codes", align_bytes=64)
-            scales = held.tile([P, n], U8, name=name + "_scales", align_bytes=64)
-            nc.vector.quantize_mx(
-                out=codes[:].bitcast(FP8X4), scales=scales[:], in_=mix.rearrange("p n t -> p (n t)")
-            )
-            return codes, scales
+        def quantise(codes, scales, mix):
+            nc.vector.quantize_mx(out=codes.bitcast(FP8X4), scales=scales, in_=mix.rearrange("p n t -> p (n t)"))
 
         def interleave(copy, mix, raw):
             copy(mix.rearrange("p (c i) t -> p c t i", i=LINE), raw.rearrange("p t (c i) -> p c t i", i=LINE))
@@ -98,26 +92,25 @@ def tile_picked_recall_gelu_e_kernel(tc, xT, sT, w1_words, w1_scales, w2_words, 
         x0_codes = held.tile([P, S], U32, name="x0_codes", align_bytes=64)
         x0_scales = held.tile([P, S], U8, name="x0_scales", align_bytes=64)
         for cols in (slice(0, HALF), slice(HALF, S)):
-            nc.vector.quantize_mx(
-                out=x0_codes[:, cols].bitcast(FP8X4),
-                scales=x0_scales[:, cols],
-                in_=x_mix0[:].rearrange("p n t -> p (n t)"),
-            )
-        x_quant = [(x0_codes, x0_scales)]
+            quantise(x0_codes[:, cols], x0_scales[:, cols], x_mix0[:])
 
         s_mix = held.tile([P, S, PACK], BF16, name="s_mix", align_bytes=64)
+        half_columns = HALF // ENTRIES
+
+        def gather_side_by_side(t):
+            picked = held.tile([P, HALF], BF16, name="picked%d" % t, align_bytes=64)
+            nc.vector.tensor_copy(s_mix[:, 0:HALF, t], planes[t][:].indirect(offsets[:, 0:half_columns]))
+            nc.scalar.activation(picked[:], planes[t][:].indirect(offsets[:, half_columns : 2 * half_columns]), COPY)
+            nc.scalar.copy(s_mix[:, HALF:S, t], picked[:])
+
         for t in range(2):
             nc.vector.tensor_copy(s_mix[:, :, t], planes[t][:].indirect(offsets[:]))
-        picked2 = held.tile([P, HALF], BF16, name="picked2", align_bytes=64)
-        half_columns = HALF // ENTRIES
-        nc.vector.tensor_copy(picked2[:], planes[2][:].indirect(offsets[:, half_columns : 2 * half_columns]))
-        nc.vector.tensor_copy(s_mix[:, 0:HALF, 2], planes[2][:].indirect(offsets[:, 0:half_columns]))
-        nc.vector.tensor_copy(s_mix[:, HALF:S, 2], picked2[:])
+        gather_side_by_side(2)
 
         turned = psum.tile([P, P], F32, name="turned", tag="acc7")
         nc.tensor.transpose(turned[:], bias_rows[:], ident[:])
         bias = held.tile([P, M_TILES], F32, name="bias")
-        nc.scalar.copy(bias[:], turned[:, 8:P:32])
+        nc.vector.tensor_copy(bias[:], turned[:, 8:P:32])
 
         unread = psum.tile([P, S], F32, name="unread", tag="acc7")
         for i in range(2):
@@ -131,34 +124,29 @@ def tile_picked_recall_gelu_e_kernel(tc, xT, sT, w1_words, w1_scales, w2_words, 
                 stop=True,
             )
 
-        picked3 = held.tile([P, HALF], BF16, name="picked", align_bytes=64)
-        nc.vector.tensor_copy(picked3[:], planes[3][:].indirect(offsets[:, half_columns : 2 * half_columns]))
-        nc.scalar.copy(s_mix[:, HALF:S, 3], picked3[:])
-        nc.vector.tensor_copy(s_mix[:, 0:HALF, 3], planes[3][:].indirect(offsets[:, 0:half_columns]))
-        s_quant = [quantise(s_mix[:, 0:HALF, :], HALF, "s0")]
-        s_quant.append(quantise(s_mix[:, HALF:S, :], HALF, "s1"))
+        gather_side_by_side(3)
+        s_codes = held.tile([P, S], U32, name="s_codes", align_bytes=64)
+        s_scales = held.tile([P, S], U8, name="s_scales", align_bytes=64)
+        for lo in (0, HALF):
+            quantise(s_codes[:, lo : lo + HALF], s_scales[:, lo : lo + HALF], s_mix[:, lo : lo + HALF, :])
 
-        late_mix = held.tile([P, HALF, PACK], BF16, name="late_mix", align_bytes=64)
         late_codes = held.tile([P, HALF], U32, name="late_codes", align_bytes=64)
         late_scales = held.tile([P, HALF], U8, name="late_scales", align_bytes=64)
 
-        def quantise_late(lo, n):
-            nc.vector.quantize_mx(
-                out=late_codes[:, lo : lo + n].bitcast(FP8X4),
-                scales=late_scales[:, lo : lo + n],
-                in_=late_mix[:, lo : lo + n, :].rearrange("p n t -> p (n t)"),
-            )
+        def late(i, lo, n):
+            c = PIECES[i][0] + lo
+            return s_mix[:, c - HALF : c - HALF + n, :], x_raw[i][:, :, lo : lo + n], slice(c - HALF, c - HALF + n)
 
-        interleave(nc.scalar.copy, late_mix[:, 0:P, :], x_raw[1][:])
-        quantise_late(0, P)
-        for lo in (0, P // 2):
-            interleave(nc.vector.tensor_copy, late_mix[:, P + lo : P + lo + P // 2, :], x_raw[2][:, :, lo : lo + P // 2])
-        for lo in (0, P // 2):
-            quantise_late(P + lo, P // 2)
-        x_quant.append((late_codes, late_scales))
+        mix, raw, cols = late(1, 0, P)
+        interleave(nc.vector.tensor_copy, mix, raw)
+        quantise(late_codes[:, cols], late_scales[:, cols], mix)
+        last = [late(2, lo, P // 2) for lo in (0, P // 2)]
+        for mix, raw, cols in last:
+            interleave(nc.vector.tensor_copy, mix, raw)
+        for mix, raw, cols in last:
+            quantise(late_codes[:, cols], late_scales[:, cols], mix)
 
-        def product(acc, words, w_scale, moving, lo, n, m, opens):
-            codes, scales = moving
+        def product(acc, words, w_scale, codes, scales, lo, n, m, opens):
             nc.tensor.matmul_mx(
                 out=acc[:],
                 lhsT=words[m].bitcast(FP8X4),
@@ -176,11 +164,12 @@ def tile_picked_recall_gelu_e_kernel(tc, xT, sT, w1_words, w1_scales, w2_words, 
         result = held.tile([P, M_TILES, S], F32, name="result")
 
         def step(m, c, n, bank):
-            half = c // HALF
-            queries = (w1_tiles, scales1, x_quant[half], c % HALF)
-            memories = (w2_tiles, scales2, s_quant[half], c % HALF)
+            memories = (w2_tiles, scales2, s_codes, s_scales, c)
+            if c < HALF:
+                first, second = (w1_tiles, scales1, x0_codes, x0_scales, c), memories
+            else:
+                first, second = memories, (w1_tiles, scales1, late_codes, late_scales, c - HALF)
             acc = psum.tile([P, n], F32, name="acc%d_%d" % (m, c), tag="acc%d" % bank)
-            first, second = (queries, memories) if half == 0 else (memories, queries)
             product(acc, *first, n, m, True)
             product(acc, *second, n, m, False)
             nc.scalar.activation(result[:, m, c : c + n], acc[:], GELU, bias=bias[:, m : m + 1])
@@ -191,10 +180,8 @@ def tile_picked_recall_gelu_e_kernel(tc, xT, sT, w1_words, w1_scales, w2_words, 
         for bank, (m, c, n) in enumerate(((0, 0, P), (0, P, P), (1, 0, HALF), (2, 0, HALF), (3, 0, HALF))):
             step(m, c, n, bank)
             store(m, m, c, n)
-        for c, banks in ((HALF, (5, 6)), (HALF + P, (7, 0))):
-            step(2, c, P, banks[0])
-            step(3, c, P, banks[1])
-            store(2, 3, c, P)
-        for m in range(2):
-            step(m, HALF, HALF, 1 + m)
-            store(m, m, HALF, HALF)
+        for c, banks in ((HALF, (5, 6, 7, 0)), (HALF + P, (1, 2, 3, 4))):
+            for m in range(M_TILES):
+                step(m, c, P, banks[m])
+                if m % 2:
+                    store(m - 1, m, c, P)

@@ -35,7 +35,7 @@ def tile_picked_recall_gelu_e_kernel(tc, xT, sT, w1_words, w1_scales, w2_words, 
         psum = ctx.enter_context(tc.psum_pool(name="psum", bufs=1))
 
         offsets = held.tile([P, S // ENTRIES], U16, name="offsets")
-        planes = [held.tile([P, T], F32, name="plane%d" % t, align_bytes=64) for t in range(PACK)]
+        planes = [held.tile([P, T], F32, name="plane%d" % t, tag="plane%d" % t, align_bytes=64) for t in range(PACK)]
         words1 = held.tile([P, N], I32, name="words1", align_bytes=64)
         words2 = [held.tile([P, HALF], I32, name="words2_%d" % i, align_bytes=64) for i in range(2)]
         w_scales = held.tile([P, N], U8, name="w_scales", align_bytes=64)
@@ -76,8 +76,8 @@ def tile_picked_recall_gelu_e_kernel(tc, xT, sT, w1_words, w1_scales, w2_words, 
         nc.sync.dma_start(planes[3][:], s_rows[:, 3, :])
         load_scale_rows(PACK, w2_scales)
         nc.sync.dma_start(words1[:], w1_rows)
-        nc.sync.dma_start(words2[0][:], w2_rows[:, 0:HALF])
         load_x(1)
+        nc.sync.dma_start(words2[0][:], w2_rows[:, 0:HALF])
         nc.sync.dma_start(words2[1][:], w2_rows[:, HALF:N])
         load_x(2)
 
@@ -124,21 +124,25 @@ def tile_picked_recall_gelu_e_kernel(tc, xT, sT, w1_words, w1_scales, w2_words, 
                 stop=True,
             )
 
-        gather_side_by_side(3)
-        s_codes = held.tile([P, S], U32, name="s_codes", align_bytes=64)
+        picked3 = held.tile([P, HALF], BF16, name="picked3", align_bytes=64)
+        nc.vector.tensor_copy(s_mix[:, 0:HALF, 3], planes[3][:].indirect(offsets[:, 0:half_columns]))
+        nc.scalar.activation(picked3[:], planes[3][:].indirect(offsets[:, half_columns : 2 * half_columns]), COPY)
+        s_codes = held.tile([P, S], U32, name="s_codes", tag="plane3", align_bytes=64)
         s_scales = held.tile([P, S], U8, name="s_scales", align_bytes=64)
-        for lo in (0, HALF):
-            quantise(s_codes[:, lo : lo + HALF], s_scales[:, lo : lo + HALF], s_mix[:, lo : lo + HALF, :])
+        nc.vector.tensor_copy(s_mix[:, HALF:S, 3], picked3[:])
+        quantise(s_codes[:, 0:HALF], s_scales[:, 0:HALF], s_mix[:, 0:HALF, :])
+        quantise(s_codes[:, HALF:S], s_scales[:, HALF:S], s_mix[:, HALF:S, :])
 
+        late_mix = held.tile([P, HALF, PACK], BF16, name="late_mix", align_bytes=64)
         late_codes = held.tile([P, HALF], U32, name="late_codes", align_bytes=64)
         late_scales = held.tile([P, HALF], U8, name="late_scales", align_bytes=64)
 
         def late(i, lo, n):
             c = PIECES[i][0] + lo
-            return s_mix[:, c - HALF : c - HALF + n, :], x_raw[i][:, :, lo : lo + n], slice(c - HALF, c - HALF + n)
+            return late_mix[:, c - HALF : c - HALF + n, :], x_raw[i][:, :, lo : lo + n], slice(c - HALF, c - HALF + n)
 
         mix, raw, cols = late(1, 0, P)
-        interleave(nc.vector.tensor_copy, mix, raw)
+        interleave(nc.scalar.copy, mix, raw)
         quantise(late_codes[:, cols], late_scales[:, cols], mix)
         last = [late(2, lo, P // 2) for lo in (0, P // 2)]
         for mix, raw, cols in last:
@@ -146,15 +150,15 @@ def tile_picked_recall_gelu_e_kernel(tc, xT, sT, w1_words, w1_scales, w2_words, 
         for mix, raw, cols in last:
             quantise(late_codes[:, cols], late_scales[:, cols], mix)
 
-        def product(acc, words, w_scale, codes, scales, lo, n, m, opens):
+        def product(acc, words, w_scale, codes, scales, lo, n, m, opens, closes):
             nc.tensor.matmul_mx(
-                out=acc[:],
+                out=acc,
                 lhsT=words[m].bitcast(FP8X4),
                 lhsT_scale=w_scale[:, m * P : (m + 1) * P],
                 rhs=codes[:, lo : lo + n].bitcast(FP8X4),
                 rhs_scale=scales[:, lo : lo + n],
                 start=opens,
-                stop=not opens,
+                stop=closes,
             )
 
         w1_tiles = [words1[:, m * P : (m + 1) * P] for m in range(M_TILES)]
@@ -163,25 +167,37 @@ def tile_picked_recall_gelu_e_kernel(tc, xT, sT, w1_words, w1_scales, w2_words, 
         out_rows = out.rearrange("(m p) n -> p m n", p=P)
         result = held.tile([P, M_TILES, S], F32, name="result")
 
-        def step(m, c, n, bank):
-            memories = (w2_tiles, scales2, s_codes, s_scales, c)
+        def queries(c):
             if c < HALF:
-                first, second = (w1_tiles, scales1, x0_codes, x0_scales, c), memories
-            else:
-                first, second = memories, (w1_tiles, scales1, late_codes, late_scales, c - HALF)
-            acc = psum.tile([P, n], F32, name="acc%d_%d" % (m, c), tag="acc%d" % bank)
-            product(acc, *first, n, m, True)
-            product(acc, *second, n, m, False)
-            nc.scalar.activation(result[:, m, c : c + n], acc[:], GELU, bias=bias[:, m : m + 1])
+                return w1_tiles, scales1, x0_codes, x0_scales, c
+            return w1_tiles, scales1, late_codes, late_scales, c - HALF
+
+        def memories(c):
+            return w2_tiles, scales2, s_codes, s_scales, c
+
+        def gelu(m, c, n, acc):
+            nc.scalar.activation(result[:, m, c : c + n], acc, GELU, bias=bias[:, m : m + 1])
+
+        def step(tiles, c, n, bank):
+            first, second = (queries(c), memories(c)) if c < HALF else (memories(c), queries(c))
+            acc = psum.tile([P, len(tiles), n], F32, name="acc%d_%d" % (tiles[0], c), tag="acc%d" % bank)
+            for i, m in enumerate(tiles):
+                product(acc[:, i, :], *first, n, m, i == 0, False)
+            for i, m in enumerate(tiles):
+                product(acc[:, i, :], *second, n, m, False, i == len(tiles) - 1)
+            for i, m in enumerate(tiles):
+                gelu(m, c, n, acc[:, i, :])
 
         def store(first, last, c, n):
             nc.sync.dma_start(out_rows[:, first : last + 1, c : c + n], result[:, first : last + 1, c : c + n])
 
         for bank, (m, c, n) in enumerate(((0, 0, P), (0, P, P), (1, 0, HALF), (2, 0, HALF), (3, 0, HALF))):
-            step(m, c, n, bank)
+            step((m,), c, n, bank)
             store(m, m, c, n)
-        for c, banks in ((HALF, (5, 6, 7, 0)), (HALF + P, (1, 2, 3, 4))):
-            for m in range(M_TILES):
-                step(m, c, P, banks[m])
-                if m % 2:
-                    store(m - 1, m, c, P)
+        for c, banks in ((HALF, (5, 6)), (HALF + P, (7, 0))):
+            step((2,), c, P, banks[0])
+            step((3,), c, P, banks[1])
+            store(2, 3, c, P)
+        for m in range(2):
+            step((m,), HALF, HALF, 1 + m)
+            store(m, m, HALF, HALF)

@@ -44,7 +44,7 @@ def tile_picked_recall_gelu_e_kernel(tc, xT, sT, w1_words, w1_scales, w2_words, 
         bias_rows = held.tile([P, P], F32, name="bias_rows")
         ident = held.tile([P, P], F32, name="ident")
         dummy = held.tile([P, 2], F32, name="dummy")
-        x_raw = [held.tile([P, PACK, n], F32, name="x_raw%d" % c, align_bytes=64) for c, n in PIECES]
+        x_raw = [held.tile([P, PACK, n], F32, name="x_raw%d" % c, tag="x_raw%d" % c, align_bytes=64) for c, n in PIECES]
 
         s_rows = sT.rearrange("(p t) c -> p t c", t=PACK)
         x_rows = xT.rearrange("(p t) n -> p t n", t=PACK)
@@ -127,11 +127,10 @@ def tile_picked_recall_gelu_e_kernel(tc, xT, sT, w1_words, w1_scales, w2_words, 
         picked3 = held.tile([P, HALF], BF16, name="picked3", align_bytes=64)
         nc.vector.tensor_copy(s_mix[:, 0:HALF, 3], planes[3][:].indirect(offsets[:, 0:half_columns]))
         nc.scalar.activation(picked3[:], planes[3][:].indirect(offsets[:, half_columns : 2 * half_columns]), COPY)
-        s_codes = held.tile([P, S], U32, name="s_codes", tag="plane3", align_bytes=64)
-        s_scales = held.tile([P, S], U8, name="s_scales", align_bytes=64)
+        first_codes = held.tile([P, HALF], U32, name="first_codes", align_bytes=64)
+        first_scales = held.tile([P, HALF], U8, name="first_scales", align_bytes=64)
+        quantise(first_codes[:], first_scales[:], s_mix[:, 0:HALF, :])
         nc.vector.tensor_copy(s_mix[:, HALF:S, 3], picked3[:])
-        quantise(s_codes[:, 0:HALF], s_scales[:, 0:HALF], s_mix[:, 0:HALF, :])
-        quantise(s_codes[:, HALF:S], s_scales[:, HALF:S], s_mix[:, HALF:S, :])
 
         late_mix = held.tile([P, HALF, PACK], BF16, name="late_mix", align_bytes=64)
         late_codes = held.tile([P, HALF], U32, name="late_codes", align_bytes=64)
@@ -144,6 +143,9 @@ def tile_picked_recall_gelu_e_kernel(tc, xT, sT, w1_words, w1_scales, w2_words, 
         mix, raw, cols = late(1, 0, P)
         interleave(nc.scalar.copy, mix, raw)
         quantise(late_codes[:, cols], late_scales[:, cols], mix)
+        second_codes = held.tile([P, HALF], U32, name="second_codes", tag="x_raw%d" % HALF, align_bytes=64)
+        second_scales = held.tile([P, HALF], U8, name="second_scales", align_bytes=64)
+        quantise(second_codes[:], second_scales[:], s_mix[:, HALF:S, :])
         last = [late(2, lo, P // 2) for lo in (0, P // 2)]
         for mix, raw, cols in last:
             interleave(nc.vector.tensor_copy, mix, raw)
@@ -173,7 +175,9 @@ def tile_picked_recall_gelu_e_kernel(tc, xT, sT, w1_words, w1_scales, w2_words, 
             return w1_tiles, scales1, late_codes, late_scales, c - HALF
 
         def memories(c):
-            return w2_tiles, scales2, s_codes, s_scales, c
+            if c < HALF:
+                return w2_tiles, scales2, first_codes, first_scales, c
+            return w2_tiles, scales2, second_codes, second_scales, c - HALF
 
         def gelu(m, c, n, acc):
             nc.scalar.activation(result[:, m, c : c + n], acc, GELU, bias=bias[:, m : m + 1])

@@ -44,7 +44,7 @@ def tile_picked_recall_gelu_e_kernel(tc, xT, sT, w1_words, w1_scales, w2_words, 
         bias_rows = held.tile([P, P], F32, name="bias_rows")
         ident = held.tile([P, P], F32, name="ident")
         dummy = held.tile([P, 2], F32, name="dummy")
-        x_raw = [held.tile([P, PACK, n], F32, name="x_raw%d" % c, tag="x_raw%d" % c, align_bytes=64) for c, n in PIECES]
+        x_raw = [held.tile([P, PACK, n], F32, name="x_raw%d" % c, align_bytes=64) for c, n in PIECES]
 
         s_rows = sT.rearrange("(p t) c -> p t c", t=PACK)
         x_rows = xT.rearrange("(p t) n -> p t n", t=PACK)
@@ -94,7 +94,8 @@ def tile_picked_recall_gelu_e_kernel(tc, xT, sT, w1_words, w1_scales, w2_words, 
         for cols in (slice(0, HALF), slice(HALF, S)):
             quantise(x0_codes[:, cols], x0_scales[:, cols], x_mix0[:])
 
-        s_mix = held.tile([P, S, PACK], BF16, name="s_mix", align_bytes=64)
+        mix = held.tile([P, S + HALF, PACK], BF16, name="mix", align_bytes=64)
+        s_mix = mix[:, 0:S, :]
         half_columns = HALF // ENTRIES
 
         def gather_side_by_side(t):
@@ -127,30 +128,25 @@ def tile_picked_recall_gelu_e_kernel(tc, xT, sT, w1_words, w1_scales, w2_words, 
         picked3 = held.tile([P, HALF], BF16, name="picked3", align_bytes=64)
         nc.vector.tensor_copy(s_mix[:, 0:HALF, 3], planes[3][:].indirect(offsets[:, 0:half_columns]))
         nc.scalar.activation(picked3[:], planes[3][:].indirect(offsets[:, half_columns : 2 * half_columns]), COPY)
-        first_codes = held.tile([P, HALF], U32, name="first_codes", align_bytes=64)
+        first_codes = held.tile([P, HALF], U32, name="first_codes", tag="plane3", align_bytes=64)
         first_scales = held.tile([P, HALF], U8, name="first_scales", align_bytes=64)
+        nc.vector.tensor_copy(s_mix[:, HALF : HALF + P, 3], picked3[:, 0:P])
         quantise(first_codes[:], first_scales[:], s_mix[:, 0:HALF, :])
-        nc.vector.tensor_copy(s_mix[:, HALF:S, 3], picked3[:])
+        nc.vector.tensor_copy(s_mix[:, HALF + P : S, 3], picked3[:, P:HALF])
 
-        late_mix = held.tile([P, HALF, PACK], BF16, name="late_mix", align_bytes=64)
-        late_codes = held.tile([P, HALF], U32, name="late_codes", align_bytes=64)
-        late_scales = held.tile([P, HALF], U8, name="late_scales", align_bytes=64)
+        late_codes = held.tile([P, S], U32, name="late_codes", align_bytes=64)
+        late_scales = held.tile([P, S], U8, name="late_scales", align_bytes=64)
 
-        def late(i, lo, n):
-            c = PIECES[i][0] + lo
-            return late_mix[:, c - HALF : c - HALF + n, :], x_raw[i][:, :, lo : lo + n], slice(c - HALF, c - HALF + n)
+        def quantise_late(c, n):
+            quantise(late_codes[:, c : c + n], late_scales[:, c : c + n], mix[:, HALF + c : HALF + c + n, :])
 
-        mix, raw, cols = late(1, 0, P)
-        interleave(nc.scalar.copy, mix, raw)
-        quantise(late_codes[:, cols], late_scales[:, cols], mix)
-        second_codes = held.tile([P, HALF], U32, name="second_codes", tag="x_raw%d" % HALF, align_bytes=64)
-        second_scales = held.tile([P, HALF], U8, name="second_scales", align_bytes=64)
-        quantise(second_codes[:], second_scales[:], s_mix[:, HALF:S, :])
-        last = [late(2, lo, P // 2) for lo in (0, P // 2)]
-        for mix, raw, cols in last:
-            interleave(nc.vector.tensor_copy, mix, raw)
-        for mix, raw, cols in last:
-            quantise(late_codes[:, cols], late_scales[:, cols], mix)
+        interleave(nc.scalar.copy, mix[:, S : S + P, :], x_raw[1][:])
+        quantise_late(0, P)
+        quantise_late(P, HALF)
+        for lo in (0, P // 2):
+            interleave(nc.vector.tensor_copy, mix[:, S + P + lo : S + P + lo + P // 2, :], x_raw[2][:, :, lo : lo + P // 2])
+        for lo in (0, P // 2):
+            quantise_late(HALF + P + lo, P // 2)
 
         def product(acc, words, w_scale, codes, scales, lo, n, m, opens, closes):
             nc.tensor.matmul_mx(
@@ -172,12 +168,12 @@ def tile_picked_recall_gelu_e_kernel(tc, xT, sT, w1_words, w1_scales, w2_words, 
         def queries(c):
             if c < HALF:
                 return w1_tiles, scales1, x0_codes, x0_scales, c
-            return w1_tiles, scales1, late_codes, late_scales, c - HALF
+            return w1_tiles, scales1, late_codes, late_scales, c
 
         def memories(c):
             if c < HALF:
                 return w2_tiles, scales2, first_codes, first_scales, c
-            return w2_tiles, scales2, second_codes, second_scales, c - HALF
+            return w2_tiles, scales2, late_codes, late_scales, c - HALF
 
         def gelu(m, c, n, acc):
             nc.scalar.activation(result[:, m, c : c + n], acc, GELU, bias=bias[:, m : m + 1])

@@ -10,12 +10,15 @@ S = 512
 N = 512
 PACK = 4
 HALF = 256
+QUARTER = 128
+EIGHTH = 64
 M_TILES = N // P
 ENTRIES = 16
 LINE = 4
+BIAS_ROW = 8
 FLOPS = 2 * 2 * K * N * S
 
-PIECES = ((0, 256), (256, 128), (384, 128))
+PIECES = ((0, HALF), (HALF, QUARTER))
 
 F32 = mybir.dt.float32
 BF16 = mybir.dt.bfloat16
@@ -45,6 +48,7 @@ def tile_picked_recall_gelu_e_kernel(tc, xT, sT, w1_words, w1_scales, w2_words, 
         ident = held.tile([P, P], F32, name="ident")
         dummy = held.tile([P, 2], F32, name="dummy")
         x_raw = [held.tile([P, PACK, n], F32, name="x_raw%d" % c, align_bytes=64) for c, n in PIECES]
+        x_last = [held.tile([P, 2, QUARTER], F32, name="x_last%d" % i, align_bytes=64) for i in range(2)]
 
         s_rows = sT.rearrange("(p t) c -> p t c", t=PACK)
         x_rows = xT.rearrange("(p t) n -> p t n", t=PACK)
@@ -72,20 +76,21 @@ def tile_picked_recall_gelu_e_kernel(tc, xT, sT, w1_words, w1_scales, w2_words, 
         load_scale_rows(0, w1_scales)
         load_x(0)
         nc.sync.dma_start(planes[2][:], s_rows[:, 2, :])
-        nc.sync.dma_start(bias_rows[8:P:32, :], b.rearrange("(m p) o -> m (p o)", p=P))
+        nc.sync.dma_start(bias_rows[BIAS_ROW:P:32, :], b.rearrange("(m p) o -> m (p o)", p=P))
         nc.sync.dma_start(planes[3][:], s_rows[:, 3, :])
         load_scale_rows(PACK, w2_scales)
         nc.sync.dma_start(words1[:], w1_rows)
         load_x(1)
         nc.sync.dma_start(words2[0][:], w2_rows[:, 0:HALF])
         nc.sync.dma_start(words2[1][:], w2_rows[:, HALF:N])
-        load_x(2)
+        for i in range(2):
+            nc.sync.dma_start(x_last[i][:], x_rows[:, 2 * i : 2 * i + 2, S - QUARTER : S])
 
-        def quantise(codes, scales, mix):
-            nc.vector.quantize_mx(out=codes.bitcast(FP8X4), scales=scales, in_=mix.rearrange("p n t -> p (n t)"))
+        def quantise(codes, scales, values):
+            nc.vector.quantize_mx(out=codes.bitcast(FP8X4), scales=scales, in_=values.rearrange("p n t -> p (n t)"))
 
-        def interleave(copy, mix, raw):
-            copy(mix.rearrange("p (c i) t -> p c t i", i=LINE), raw.rearrange("p t (c i) -> p c t i", i=LINE))
+        def interleave(copy, places, raw):
+            copy(places.rearrange("p (c i) t -> p c t i", i=LINE), raw.rearrange("p t (c i) -> p c t i", i=LINE))
 
         x_mix0 = held.tile([P, HALF, PACK], BF16, name="x_mix0", align_bytes=64)
         interleave(nc.scalar.copy, x_mix0[:], x_raw[0][:])
@@ -96,22 +101,23 @@ def tile_picked_recall_gelu_e_kernel(tc, xT, sT, w1_words, w1_scales, w2_words, 
 
         mix = held.tile([P, S + HALF, PACK], BF16, name="mix", align_bytes=64)
         s_mix = mix[:, 0:S, :]
-        half_columns = HALF // ENTRIES
+        first_entries = offsets[:, 0 : HALF // ENTRIES]
+        second_entries = offsets[:, HALF // ENTRIES : S // ENTRIES]
 
         def gather_side_by_side(t):
             picked = held.tile([P, HALF], BF16, name="picked%d" % t, align_bytes=64)
-            nc.vector.tensor_copy(s_mix[:, 0:HALF, t], planes[t][:].indirect(offsets[:, 0:half_columns]))
-            nc.scalar.activation(picked[:], planes[t][:].indirect(offsets[:, half_columns : 2 * half_columns]), COPY)
-            nc.scalar.copy(s_mix[:, HALF:S, t], picked[:])
+            nc.vector.tensor_copy(s_mix[:, 0:HALF, t], planes[t][:].indirect(first_entries))
+            nc.scalar.activation(picked[:], planes[t][:].indirect(second_entries), COPY)
+            return picked
 
         for t in range(2):
             nc.vector.tensor_copy(s_mix[:, :, t], planes[t][:].indirect(offsets[:]))
-        gather_side_by_side(2)
+        nc.scalar.copy(s_mix[:, HALF:S, 2], gather_side_by_side(2)[:])
 
         turned = psum.tile([P, P], F32, name="turned", tag="acc7")
         nc.tensor.transpose(turned[:], bias_rows[:], ident[:])
         bias = held.tile([P, M_TILES], F32, name="bias")
-        nc.vector.tensor_copy(bias[:], turned[:, 8:P:32])
+        nc.vector.tensor_copy(bias[:], turned[:, BIAS_ROW:P:32])
 
         unread = psum.tile([P, S], F32, name="unread", tag="acc7")
         for i in range(2):
@@ -125,14 +131,12 @@ def tile_picked_recall_gelu_e_kernel(tc, xT, sT, w1_words, w1_scales, w2_words, 
                 stop=True,
             )
 
-        picked3 = held.tile([P, HALF], BF16, name="picked3", align_bytes=64)
-        nc.vector.tensor_copy(s_mix[:, 0:HALF, 3], planes[3][:].indirect(offsets[:, 0:half_columns]))
-        nc.scalar.activation(picked3[:], planes[3][:].indirect(offsets[:, half_columns : 2 * half_columns]), COPY)
+        picked3 = gather_side_by_side(3)
         first_codes = held.tile([P, HALF], U32, name="first_codes", tag="plane3", align_bytes=64)
         first_scales = held.tile([P, HALF], U8, name="first_scales", align_bytes=64)
-        nc.vector.tensor_copy(s_mix[:, HALF : HALF + P, 3], picked3[:, 0:P])
+        nc.vector.tensor_copy(s_mix[:, HALF : HALF + QUARTER, 3], picked3[:, 0:QUARTER])
         quantise(first_codes[:], first_scales[:], s_mix[:, 0:HALF, :])
-        nc.vector.tensor_copy(s_mix[:, HALF + P : S, 3], picked3[:, P:HALF])
+        nc.vector.tensor_copy(s_mix[:, HALF + QUARTER : S, 3], picked3[:, QUARTER:HALF])
 
         late_codes = held.tile([P, S], U32, name="late_codes", align_bytes=64)
         late_scales = held.tile([P, S], U8, name="late_scales", align_bytes=64)
@@ -140,64 +144,56 @@ def tile_picked_recall_gelu_e_kernel(tc, xT, sT, w1_words, w1_scales, w2_words, 
         def quantise_late(c, n):
             quantise(late_codes[:, c : c + n], late_scales[:, c : c + n], mix[:, HALF + c : HALF + c + n, :])
 
-        interleave(nc.scalar.copy, mix[:, S : S + P, :], x_raw[1][:])
-        quantise_late(0, P)
-        quantise_late(P, HALF)
-        for lo in (0, P // 2):
-            interleave(nc.vector.tensor_copy, mix[:, S + P + lo : S + P + lo + P // 2, :], x_raw[2][:, :, lo : lo + P // 2])
-        for lo in (0, P // 2):
-            quantise_late(HALF + P + lo, P // 2)
+        interleave(nc.scalar.copy, mix[:, S : S + QUARTER, :], x_raw[1][:])
+        quantise_late(0, QUARTER)
+        quantise_late(QUARTER, HALF)
+        last_mix = mix[:, S + QUARTER : S + HALF, :]
+        interleave(nc.vector.tensor_copy, last_mix[:, :, 0:2], x_last[0][:])
+        for lo in (0, EIGHTH):
+            interleave(nc.vector.tensor_copy, last_mix[:, lo : lo + EIGHTH, 2:PACK], x_last[1][:, :, lo : lo + EIGHTH])
+        for lo in (0, EIGHTH):
+            quantise_late(HALF + QUARTER + lo, EIGHTH)
 
-        def product(acc, words, w_scale, codes, scales, lo, n, m, opens, closes):
+        w1_tiles = [words1[:, m * P : (m + 1) * P] for m in range(M_TILES)]
+        w2_tiles = [words2[m // 2][:, m % 2 * P : (m % 2 + 1) * P] for m in range(M_TILES)]
+
+        def product(acc, words, w_scale, codes, scales, lo, n, m, opens):
             nc.tensor.matmul_mx(
-                out=acc,
+                out=acc[:],
                 lhsT=words[m].bitcast(FP8X4),
                 lhsT_scale=w_scale[:, m * P : (m + 1) * P],
                 rhs=codes[:, lo : lo + n].bitcast(FP8X4),
                 rhs_scale=scales[:, lo : lo + n],
                 start=opens,
-                stop=closes,
+                stop=not opens,
             )
-
-        w1_tiles = [words1[:, m * P : (m + 1) * P] for m in range(M_TILES)]
-        w2_tiles = [words2[m // 2][:, m % 2 * P : (m % 2 + 1) * P] for m in range(M_TILES)]
 
         out_rows = out.rearrange("(m p) n -> p m n", p=P)
         result = held.tile([P, M_TILES, S], F32, name="result")
 
-        def queries(c):
+        def step(m, c, n, bank):
             if c < HALF:
-                return w1_tiles, scales1, x0_codes, x0_scales, c
-            return w1_tiles, scales1, late_codes, late_scales, c
-
-        def memories(c):
-            if c < HALF:
-                return w2_tiles, scales2, first_codes, first_scales, c
-            return w2_tiles, scales2, late_codes, late_scales, c - HALF
-
-        def gelu(m, c, n, acc):
-            nc.scalar.activation(result[:, m, c : c + n], acc, GELU, bias=bias[:, m : m + 1])
-
-        def step(tiles, c, n, bank):
-            first, second = (queries(c), memories(c)) if c < HALF else (memories(c), queries(c))
-            acc = psum.tile([P, len(tiles), n], F32, name="acc%d_%d" % (tiles[0], c), tag="acc%d" % bank)
-            for i, m in enumerate(tiles):
-                product(acc[:, i, :], *first, n, m, i == 0, False)
-            for i, m in enumerate(tiles):
-                product(acc[:, i, :], *second, n, m, False, i == len(tiles) - 1)
-            for i, m in enumerate(tiles):
-                gelu(m, c, n, acc[:, i, :])
+                first = (w1_tiles, scales1, x0_codes, x0_scales, c)
+                second = (w2_tiles, scales2, first_codes, first_scales, c)
+            else:
+                first = (w2_tiles, scales2, late_codes, late_scales, c - HALF)
+                second = (w1_tiles, scales1, late_codes, late_scales, c)
+            acc = psum.tile([P, n], F32, name="acc%d_%d" % (m, c), tag="acc%d" % bank)
+            product(acc, *first, n, m, True)
+            product(acc, *second, n, m, False)
+            nc.scalar.activation(result[:, m, c : c + n], acc[:], GELU, bias=bias[:, m : m + 1])
 
         def store(first, last, c, n):
             nc.sync.dma_start(out_rows[:, first : last + 1, c : c + n], result[:, first : last + 1, c : c + n])
 
-        for bank, (m, c, n) in enumerate(((0, 0, P), (0, P, P), (1, 0, HALF), (2, 0, HALF), (3, 0, HALF))):
-            step((m,), c, n, bank)
+        first_half = ((0, 0, QUARTER), (0, QUARTER, QUARTER), (1, 0, HALF), (2, 0, HALF), (3, 0, HALF))
+        for bank, (m, c, n) in enumerate(first_half):
+            step(m, c, n, bank)
             store(m, m, c, n)
-        for c, banks in ((HALF, (5, 6)), (HALF + P, (7, 0))):
-            step((2,), c, P, banks[0])
-            step((3,), c, P, banks[1])
-            store(2, 3, c, P)
+        for c, banks in ((HALF, (5, 6)), (HALF + QUARTER, (7, 0))):
+            step(2, c, QUARTER, banks[0])
+            step(3, c, QUARTER, banks[1])
+            store(2, 3, c, QUARTER)
         for m in range(2):
-            step((m,), HALF, HALF, 1 + m)
+            step(m, HALF, HALF, 1 + m)
             store(m, m, HALF, HALF)

@@ -14,6 +14,7 @@ QUARTER = 128
 EIGHTH = 64
 M_TILES = N // P
 ENTRIES = 16
+ROW_ALIGN = 256
 LINE = 4
 BIAS_ROW = 8
 FLOPS = 2 * 2 * K * N * S
@@ -38,17 +39,17 @@ def tile_picked_recall_gelu_e_kernel(tc, xT, sT, w1_words, w1_scales, w2_words, 
         psum = ctx.enter_context(tc.psum_pool(name="psum", bufs=1))
 
         offsets = held.tile([P, S // ENTRIES], U16, name="offsets")
-        planes = [held.tile([P, T], F32, name="plane%d" % t, tag="plane%d" % t, align_bytes=64) for t in range(PACK)]
-        words1 = held.tile([P, N], I32, name="words1", align_bytes=64)
-        words2 = [held.tile([P, HALF], I32, name="words2_%d" % i, align_bytes=64) for i in range(2)]
-        w_scales = held.tile([P, N], U8, name="w_scales", align_bytes=64)
+        planes = [held.tile([P, T], F32, name="plane%d" % t, tag="plane%d" % t, align_bytes=ROW_ALIGN) for t in range(PACK)]
+        words1 = held.tile([P, N], I32, name="words1", align_bytes=ROW_ALIGN)
+        words2 = [held.tile([P, HALF], I32, name="words2_%d" % i, align_bytes=ROW_ALIGN) for i in range(2)]
+        w_scales = held.tile([P, N], U8, name="w_scales", align_bytes=ROW_ALIGN)
         scales1 = w_scales[:, :]
         scales2 = w_scales[PACK:P, :]
-        bias_rows = held.tile([P, P], F32, name="bias_rows")
+        bias_rows = held.tile([P, P], F32, name="bias_rows", align_bytes=ROW_ALIGN)
         ident = held.tile([P, P], F32, name="ident")
         dummy = held.tile([P, 2], F32, name="dummy")
-        x_raw = [held.tile([P, PACK, n], F32, name="x_raw%d" % c, align_bytes=64) for c, n in PIECES]
-        x_last = [held.tile([P, 2, QUARTER], F32, name="x_last%d" % i, align_bytes=64) for i in range(2)]
+        x_raw = [held.tile([P, PACK, n], F32, name="x_raw%d" % c, align_bytes=ROW_ALIGN) for c, n in PIECES]
+        x_last = [held.tile([P, 2, QUARTER], F32, name="x_last%d" % i, align_bytes=ROW_ALIGN) for i in range(2)]
 
         s_rows = sT.rearrange("(p t) c -> p t c", t=PACK)
         x_rows = xT.rearrange("(p t) n -> p t n", t=PACK)
@@ -132,7 +133,7 @@ def tile_picked_recall_gelu_e_kernel(tc, xT, sT, w1_words, w1_scales, w2_words, 
             )
 
         picked3 = gather_side_by_side(3)
-        first_codes = held.tile([P, HALF], U32, name="first_codes", tag="plane3", align_bytes=64)
+        first_codes = held.tile([P, HALF], U32, name="first_codes", tag="plane3", align_bytes=ROW_ALIGN)
         first_scales = held.tile([P, HALF], U8, name="first_scales", align_bytes=64)
         nc.vector.tensor_copy(s_mix[:, HALF : HALF + QUARTER, 3], picked3[:, 0:QUARTER])
         quantise(first_codes[:], first_scales[:], s_mix[:, 0:HALF, :])
@@ -169,7 +170,7 @@ def tile_picked_recall_gelu_e_kernel(tc, xT, sT, w1_words, w1_scales, w2_words, 
             )
 
         out_rows = out.rearrange("(m p) n -> p m n", p=P)
-        result = held.tile([P, M_TILES, S], F32, name="result")
+        result = held.tile([P, M_TILES, S], F32, name="result", align_bytes=ROW_ALIGN)
 
         def step(m, c, n, bank):
             if c < HALF:

@@ -15,6 +15,8 @@ EIGHTH = 64
 M_TILES = N // P
 ENTRIES = 16
 ROW_ALIGN = 256
+QUADRANT = 32
+HOME = 2
 LINE = 4
 BIAS_ROW = 8
 FLOPS = 2 * 2 * K * N * S
@@ -42,9 +44,10 @@ def tile_picked_recall_gelu_e_kernel(tc, xT, sT, w1_words, w1_scales, w2_words, 
         planes = [held.tile([P, T], F32, name="plane%d" % t, tag="plane%d" % t, align_bytes=ROW_ALIGN) for t in range(PACK)]
         words1 = held.tile([P, N], I32, name="words1", align_bytes=ROW_ALIGN)
         words2 = [held.tile([P, HALF], I32, name="words2_%d" % i, align_bytes=ROW_ALIGN) for i in range(2)]
-        w_scales = held.tile([P, N], U8, name="w_scales", align_bytes=ROW_ALIGN)
-        scales1 = w_scales[:, :]
-        scales2 = w_scales[PACK:P, :]
+        staged = [held.tile([P, PACK * N], U8, name="staged%d" % i, align_bytes=ROW_ALIGN) for i in range(2)]
+        slots = [tile[:].bitcast(I32).rearrange("p (q c) -> p q c", q=PACK) for tile in staged]
+        scales1 = staged[0][:, HOME * N : (HOME + 1) * N]
+        scales2 = staged[1][PACK:P, HOME * N : (HOME + 1) * N]
         bias_rows = held.tile([P, P], F32, name="bias_rows", align_bytes=ROW_ALIGN)
         ident = held.tile([P, P], F32, name="ident")
         dummy = held.tile([P, 2], F32, name="dummy")
@@ -56,14 +59,21 @@ def tile_picked_recall_gelu_e_kernel(tc, xT, sT, w1_words, w1_scales, w2_words, 
         w1_rows = w1_words[0].rearrange("p m r -> p (m r)").bitcast(I32)
         w2_rows = w2_words[0].rearrange("p m r -> p (m r)").bitcast(I32)
 
-        nc.gpsimd.memset(w_scales[:].bitcast(I32), 0)
+        landing = slice(HOME * QUADRANT, (HOME + 1) * QUADRANT)
+        for tile in staged:
+            nc.vector.memset(tile[landing, :].bitcast(I32), 0)
         nc.gpsimd.memset(bias_rows[:], 0.0)
         nc.vector.memset(dummy[:], 0.0)
         make_identity(nc, ident[:])
 
-        def load_scale_rows(first, source):
-            for r in range(PACK):
-                nc.sync.dma_start(w_scales[first + r : P : 32, :].bitcast(I32), source[0, r:16:PACK, :].bitcast(I32))
+        def load_scale_rows(i, source):
+            first = HOME * QUADRANT + PACK * i
+            nc.sync.dma_start(slots[i][first : first + PACK], source[0].bitcast(I32).rearrange("(q r) c -> r q c", r=PACK))
+
+        def spread_scale_rows(i):
+            for q in range(PACK):
+                if q != HOME:
+                    nc.vector.tensor_copy(slots[i][q * QUADRANT : (q + 1) * QUADRANT, HOME, :], slots[i][landing, q, :])
 
         def load_x(i):
             c, n = PIECES[i]
@@ -73,19 +83,22 @@ def tile_picked_recall_gelu_e_kernel(tc, xT, sT, w1_words, w1_scales, w2_words, 
 
         nc.sync.dma_start(planes[0][:], s_rows[:, 0, :])
         nc.sync.dma_start(offsets[:], offs)
-        nc.sync.dma_start(planes[1][:], s_rows[:, 1, :])
         load_scale_rows(0, w1_scales)
+        load_scale_rows(1, w2_scales)
+        nc.sync.dma_start(planes[1][:], s_rows[:, 1, :])
         load_x(0)
         nc.sync.dma_start(planes[2][:], s_rows[:, 2, :])
         nc.sync.dma_start(bias_rows[BIAS_ROW:P:32, :], b.rearrange("(m p) o -> m (p o)", p=P))
         nc.sync.dma_start(planes[3][:], s_rows[:, 3, :])
-        load_scale_rows(PACK, w2_scales)
         nc.sync.dma_start(words1[:], w1_rows)
         load_x(1)
         nc.sync.dma_start(words2[0][:], w2_rows[:, 0:HALF])
         nc.sync.dma_start(words2[1][:], w2_rows[:, HALF:N])
         for i in range(2):
             nc.sync.dma_start(x_last[i][:], x_rows[:, 2 * i : 2 * i + 2, S - QUARTER : S])
+
+        for i in range(2):
+            spread_scale_rows(i)
 
         def quantise(codes, scales, values):
             nc.vector.quantize_mx(out=codes.bitcast(FP8X4), scales=scales, in_=values.rearrange("p n t -> p (n t)"))
@@ -111,9 +124,9 @@ def tile_picked_recall_gelu_e_kernel(tc, xT, sT, w1_words, w1_scales, w2_words, 
             nc.scalar.activation(picked[:], planes[t][:].indirect(second_entries), COPY)
             return picked
 
-        for t in range(2):
-            nc.vector.tensor_copy(s_mix[:, :, t], planes[t][:].indirect(offsets[:]))
-        nc.scalar.copy(s_mix[:, HALF:S, 2], gather_side_by_side(2)[:])
+        for t in range(3):
+            nc.vector.tensor_copy(s_mix[:, 0:HALF, t], planes[t][:].indirect(first_entries))
+            nc.scalar.activation(s_mix[:, HALF:S, t], planes[t][:].indirect(second_entries), COPY)
 
         turned = psum.tile([P, P], F32, name="turned", tag="acc7")
         nc.tensor.transpose(turned[:], bias_rows[:], ident[:])

from contextlib import ExitStack

import concourse.mybir as mybir
from concourse.masks import make_identity

P = 128
K = 512
T = 2048
S = 512
N = 512
PACK = 4
HALF = 256
QUARTER = 128
EIGHTH = 64
M_TILES = N // P
ENTRIES = 16
ROW_ALIGN = 256
QUADRANT = 32
HOME = 2
LINE = 4
BIAS_ROW = 8
FLOPS = 2 * 2 * K * N * S

PIECES = ((0, HALF), (HALF, QUARTER))

F32 = mybir.dt.float32
BF16 = mybir.dt.bfloat16
I32 = mybir.dt.int32
U32 = mybir.dt.uint32
U16 = mybir.dt.uint16
U8 = mybir.dt.uint8
FP8X4 = mybir.dt.float8_e4m3fn_x4
GELU = mybir.ActivationFunctionType.Gelu_apprx_tanh
COPY = mybir.ActivationFunctionType.Copy


def tile_picked_recall_gelu_e_kernel(tc, xT, sT, w1_words, w1_scales, w2_words, w2_scales, b, offs, out):
    nc = tc.nc
    with ExitStack() as ctx:
        held = ctx.enter_context(tc.tile_pool(name="held", bufs=1))
        psum = ctx.enter_context(tc.psum_pool(name="psum", bufs=1))

        offsets = held.tile([P, S // ENTRIES], U16, name="offsets")
        planes = [held.tile([P, T], F32, name="plane%d" % t, tag="plane%d" % t, align_bytes=ROW_ALIGN) for t in range(PACK)]
        words1 = held.tile([P, N], I32, name="words1", align_bytes=ROW_ALIGN)
        words2 = [held.tile([P, HALF], I32, name="words2_%d" % i, align_bytes=ROW_ALIGN) for i in range(2)]
        staged = [held.tile([P, PACK * N], U8, name="staged%d" % i, align_bytes=ROW_ALIGN) for i in range(2)]
        slots = [tile[:].bitcast(I32).rearrange("p (q c) -> p q c", q=PACK) for tile in staged]
        scales1 = staged[0][:, HOME * N : (HOME + 1) * N]
        scales2 = staged[1][PACK:P, HOME * N : (HOME + 1) * N]
        bias_rows = held.tile([P, P], F32, name="bias_rows", align_bytes=ROW_ALIGN)
        ident = held.tile([P, P], F32, name="ident")
        dummy = held.tile([P, 2], F32, name="dummy")
        x_raw = [held.tile([P, PACK, n], F32, name="x_raw%d" % c, align_bytes=ROW_ALIGN) for c, n in PIECES]
        x_last = [held.tile([P, 2, QUARTER], F32, name="x_last%d" % i, align_bytes=ROW_ALIGN) for i in range(2)]

        s_rows = sT.rearrange("(p t) c -> p t c", t=PACK)
        x_rows = xT.rearrange("(p t) n -> p t n", t=PACK)
        w1_rows = w1_words[0].rearrange("p m r -> p (m r)").bitcast(I32)
        w2_rows = w2_words[0].rearrange("p m r -> p (m r)").bitcast(I32)

        landing = slice(HOME * QUADRANT, (HOME + 1) * QUADRANT)
        for tile in staged:
            nc.vector.memset(tile[landing, :].bitcast(I32), 0)
        nc.gpsimd.memset(bias_rows[:], 0.0)
        nc.vector.memset(dummy[:], 0.0)
        make_identity(nc, ident[:])

        def load_scale_rows(i, source):
            first = HOME * QUADRANT + PACK * i
            nc.sync.dma_start(slots[i][first : first + PACK], source[0].bitcast(I32).rearrange("(q r) c -> r q c", r=PACK))

        def spread_scale_rows(i):
            for q in range(PACK):
                if q != HOME:
                    nc.vector.tensor_copy(slots[i][q * QUADRANT : (q + 1) * QUADRANT, HOME, :], slots[i][landing, q, :])

        def load_x(i):
            c, n = PIECES[i]
            nc.sync.dma_start(x_raw[i][:], x_rows[:, :, c : c + n])

        nc.scalar.activation(dummy[:, 1:2], dummy[:, 0:1], GELU)

        nc.sync.dma_start(planes[0][:], s_rows[:, 0, :])
        nc.sync.dma_start(offsets[:], offs)
        load_scale_rows(0, w1_scales)
        load_scale_rows(1, w2_scales)
        nc.sync.dma_start(planes[1][:], s_rows[:, 1, :])
        load_x(0)
        nc.sync.dma_start(planes[2][:], s_rows[:, 2, :])
        nc.sync.dma_start(bias_rows[BIAS_ROW:P:32, :], b.rearrange("(m p) o -> m (p o)", p=P))
        nc.sync.dma_start(planes[3][:], s_rows[:, 3, :])
        nc.sync.dma_start(words1[:], w1_rows)
        load_x(1)
        nc.sync.dma_start(words2[0][:], w2_rows[:, 0:HALF])
        nc.sync.dma_start(words2[1][:], w2_rows[:, HALF:N])
        for i in range(2):
            nc.sync.dma_start(x_last[i][:], x_rows[:, 2 * i : 2 * i + 2, S - QUARTER : S])

        for i in range(2):
            spread_scale_rows(i)

        def quantise(codes, scales, values):
            nc.vector.quantize_mx(out=codes.bitcast(FP8X4), scales=scales, in_=values.rearrange("p n t -> p (n t)"))

        def interleave(copy, places, raw):
            copy(places.rearrange("p (c i) t -> p c t i", i=LINE), raw.rearrange("p t (c i) -> p c t i", i=LINE))

        x_mix0 = held.tile([P, HALF, PACK], BF16, name="x_mix0", align_bytes=64)
        interleave(nc.scalar.copy, x_mix0[:], x_raw[0][:])
        x0_codes = held.tile([P, S], U32, name="x0_codes", align_bytes=64)
        x0_scales = held.tile([P, S], U8, name="x0_scales", align_bytes=64)
        for cols in (slice(0, HALF), slice(HALF, S)):
            quantise(x0_codes[:, cols], x0_scales[:, cols], x_mix0[:])

        mix = held.tile([P, S + HALF, PACK], BF16, name="mix", align_bytes=64)
        s_mix = mix[:, 0:S, :]
        first_entries = offsets[:, 0 : HALF // ENTRIES]
        second_entries = offsets[:, HALF // ENTRIES : S // ENTRIES]

        def gather_side_by_side(t):
            picked = held.tile([P, HALF], BF16, name="picked%d" % t, align_bytes=64)
            nc.vector.tensor_copy(s_mix[:, 0:HALF, t], planes[t][:].indirect(first_entries))
            nc.scalar.activation(picked[:], planes[t][:].indirect(second_entries), COPY)
            return picked

        for t in range(3):
            nc.vector.tensor_copy(s_mix[:, 0:HALF, t], planes[t][:].indirect(first_entries))
            nc.scalar.activation(s_mix[:, HALF:S, t], planes[t][:].indirect(second_entries), COPY)

        turned = psum.tile([P, P], F32, name="turned", tag="acc7")
        nc.tensor.transpose(turned[:], bias_rows[:], ident[:])
        bias = held.tile([P, M_TILES], F32, name="bias")
        nc.vector.tensor_copy(bias[:], turned[:, BIAS_ROW:P:32])

        unread = psum.tile([P, S], F32, name="unread", tag="acc7")
        for i in range(2):
            nc.tensor.matmul_mx(
                out=unread[:],
                lhsT=x0_codes[:, 0:P].bitcast(FP8X4),
                lhsT_scale=x0_scales[:, 0:P],
                rhs=x0_codes[:].bitcast(FP8X4),
                rhs_scale=x0_scales[:],
                start=True,
                stop=True,
            )

        picked3 = gather_side_by_side(3)
        first_codes = held.tile([P, HALF], U32, name="first_codes", tag="plane3", align_bytes=ROW_ALIGN)
        first_scales = held.tile([P, HALF], U8, name="first_scales", align_bytes=64)
        nc.vector.tensor_copy(s_mix[:, HALF : HALF + QUARTER, 3], picked3[:, 0:QUARTER])
        quantise(first_codes[:], first_scales[:], s_mix[:, 0:HALF, :])
        nc.vector.tensor_copy(s_mix[:, HALF + QUARTER : S, 3], picked3[:, QUARTER:HALF])

        late_codes = held.tile([P, S], U32, name="late_codes", align_bytes=64)
        late_scales = held.tile([P, S], U8, name="late_scales", align_bytes=64)

        def quantise_late(c, n):
            quantise(late_codes[:, c : c + n], late_scales[:, c : c + n], mix[:, HALF + c : HALF + c + n, :])

        interleave(nc.scalar.copy, mix[:, S : S + QUARTER, :], x_raw[1][:])
        quantise_late(0, QUARTER)
        quantise_late(QUARTER, HALF)
        last_mix = mix[:, S + QUARTER : S + HALF, :]
        interleave(nc.vector.tensor_copy, last_mix[:, :, 0:2], x_last[0][:])
        for lo in (0, EIGHTH):
            interleave(nc.vector.tensor_copy, last_mix[:, lo : lo + EIGHTH, 2:PACK], x_last[1][:, :, lo : lo + EIGHTH])
        for lo in (0, EIGHTH):
            quantise_late(HALF + QUARTER + lo, EIGHTH)

        w1_tiles = [words1[:, m * P : (m + 1) * P] for m in range(M_TILES)]
        w2_tiles = [words2[m // 2][:, m % 2 * P : (m % 2 + 1) * P] for m in range(M_TILES)]

        def product(acc, words, w_scale, codes, scales, lo, n, m, opens):
            nc.tensor.matmul_mx(
                out=acc[:],
                lhsT=words[m].bitcast(FP8X4),
                lhsT_scale=w_scale[:, m * P : (m + 1) * P],
                rhs=codes[:, lo : lo + n].bitcast(FP8X4),
                rhs_scale=scales[:, lo : lo + n],
                start=opens,
                stop=not opens,
            )

        out_rows = out.rearrange("(m p) n -> p m n", p=P)
        result = held.tile([P, M_TILES, S], F32, name="result", align_bytes=ROW_ALIGN)

        def step(m, c, n, bank):
            if c < HALF:
                first = (w1_tiles, scales1, x0_codes, x0_scales, c)
                second = (w2_tiles, scales2, first_codes, first_scales, c)
            else:
                first = (w2_tiles, scales2, late_codes, late_scales, c - HALF)
                second = (w1_tiles, scales1, late_codes, late_scales, c)
            acc = psum.tile([P, n], F32, name="acc%d_%d" % (m, c), tag="acc%d" % bank)
            product(acc, *first, n, m, True)
            product(acc, *second, n, m, False)
            nc.scalar.activation(result[:, m, c : c + n], acc[:], GELU, bias=bias[:, m : m + 1])

        def store(first, last, c, n):
            nc.sync.dma_start(out_rows[:, first : last + 1, c : c + n], result[:, first : last + 1, c : c + n])

        first_half = ((0, 0, QUARTER), (0, QUARTER, QUARTER), (1, 0, HALF), (2, 0, HALF), (3, 0, HALF))
        for bank, (m, c, n) in enumerate(first_half):
            step(m, c, n, bank)
            store(m, m, c, n)
        for c, banks in ((HALF, (5, 6)), (HALF + QUARTER, (7, 0))):
            step(2, c, QUARTER, banks[0])
            step(3, c, QUARTER, banks[1])
            store(2, 3, c, QUARTER)
        for m in range(2):
            step(m, HALF, HALF, 1 + m)
            store(m, m, HALF, HALF)
